import numpy as np
import ml_dtypes


def mxq(x, axis, fmt="e4m3"):
    dtype, down = {"e4m3": (ml_dtypes.float8_e4m3fn, 7), "e5m2": (ml_dtypes.float8_e5m2, 14)}[fmt]
    v = np.moveaxis(np.asarray(x, np.float32).astype(ml_dtypes.bfloat16).astype(np.float64), axis, -1)
    blocks = v.reshape(v.shape[:-1] + (-1, 32))
    amax = np.abs(blocks).max(-1, keepdims=True)
    byte = np.maximum(np.where(amax > 0, np.frexp(amax)[1] - 1 + 127, 0) - down, 1)
    scale = np.exp2(byte - 127.0)
    codes = (blocks / scale).astype(np.float32).astype(dtype).astype(np.float64)
    return np.moveaxis((codes * scale).reshape(v.shape), -1, axis)


WIDE = False


def mx_kscale(k):
    if not WIDE:
        return np.ones(k)
    levels = np.array([10, -10, 5, -5, 0])
    if k % 512:
        return np.exp2(np.random.permutation(np.resize(levels, k // 32))).repeat(32)
    a = np.empty((k // 512, 16))
    for p in range(k // 512):
        a[p, :8] = np.random.permutation(np.resize(levels, 8))
        for g in range(8):
            far = levels[np.abs(levels - a[p, g]) >= 10]
            a[p, g + 8] = far[np.random.randint(len(far))]
    return np.exp2(a.ravel()).repeat(32)


def f64(x):
    return np.asarray(x).astype(np.float64)


def striped8(idx):
    return np.concatenate([x.reshape(-1, 16).T for x in idx]).astype(np.uint16)


def runs(offs, k):
    lists = np.stack([offs[16 * r : 16 * r + 16].T.reshape(-1) for r in range(8)]).astype(np.int64)
    return lists[np.arange(k) % 512 // 64]


def pack_weight(w):
    k, n = w.shape
    w = f64(np.asarray(w, np.float32).astype(ml_dtypes.bfloat16)).reshape(k // 32, 32, n)
    amax = np.abs(w).max(1)
    byte = np.clip(np.where(amax > 0, np.frexp(amax)[1] - 1 + 127 - 7, 1), 1, 254)
    scaled = (w * np.exp2(127.0 - byte)[:, None, :]).reshape(k, n).astype(np.float32)
    words = np.ascontiguousarray(scaled.reshape(k // 512, 128, 4, n).transpose(0, 1, 3, 2)).astype(ml_dtypes.float8_e4m3fn).view(np.uint8)
    return words, np.ascontiguousarray(byte.astype(np.uint8).reshape(k // 512, 16, n))


def unpack_weight(words, scales):
    g, p, n, _ = words.shape
    vals = np.ascontiguousarray(words).view(ml_dtypes.float8_e4m3fn).astype(np.float64) * np.repeat(np.exp2(scales.astype(np.float64) - 127.0), 8, axis=1)[..., None]
    return vals.transpose(0, 1, 3, 2).reshape(g * 512, n)


def sigmoid(v):
    return 1.0 / (1.0 + np.exp(-np.maximum(v, -700.0)))


K, T, S, N, H, U = 512, 2048, 512, 512, 512, 1024


def setup_inputs():
    n = np.random.standard_normal
    s = mx_kscale(K)[:, None]
    u = mx_kscale(H)
    packed_xT = pack_weight(n((K, T)) * s)
    return {
        "x_words": packed_xT[0],
        "x_scales": packed_xT[1],
        "w1": (n((K, H)) / np.sqrt(K) / s).astype(np.float32),
        "mem": n((H, U)).astype(np.float32),
        "gn": (np.random.uniform(0.5, 1.5, (H, 1)) * u[:, None]).astype(np.float32),
        "w2": (n((H, N)) / np.sqrt(H) / u[:, None]).astype(np.float32),
        "offs": striped8(np.random.randint(0, T, (8, S))),
        "a1": striped8(np.random.randint(0, U, (8, S))),
        "a2": striped8(np.random.randint(0, U, (8, S))),
    }


def reference(x_words, x_scales, w1, mem, gn, w2, offs, a1, a2):
    xq = unpack_weight(x_words, x_scales)[np.arange(K)[:, None], runs(offs, K)]
    y = mxq(f64(w1), 0, "e4m3").T @ xq
    h = y + sigmoid(y) * (f64(mem)[np.arange(H)[:, None], runs(a1, H)])
    z = f64(gn) * (h + sigmoid(h) * (f64(mem)[np.arange(H)[:, None], runs(a2, H)]))
    return mxq(f64(w2), 0, "e4m3").T @ mxq(z, 0, "e4m3")

@@ -1,0 +1,227 @@
+from contextlib import ExitStack
+
+import concourse.mybir as mybir
+
+F32 = mybir.dt.float32
+BF16 = mybir.dt.bfloat16
+I32 = mybir.dt.int32
+U32 = mybir.dt.uint32
+U16 = mybir.dt.uint16
+U8 = mybir.dt.uint8
+FP8X4 = mybir.dt.float8_e4m3fn_x4
+MULT = mybir.AluOpType.mult
+ADD = mybir.AluOpType.add
+SIGMOID = mybir.ActivationFunctionType.Sigmoid
+COPY = mybir.ActivationFunctionType.Copy
+
+P = 128
+PACK = 4
+T, S, H, N, U = 2048, 512, 512, 512, 1024
+FLOPS = 2 * 512 * H * S + 2 * H * N * S
+CHUNKS = ((0, 256), (256, 256))
+STRADDLE = 14
+MOVED = 112
+
+
+def tile_picked_memhop2_none_p_kernel(
+    tc, x_words, x_scales, w1, mem, gn, w2, offs, a1, a2, out
+):
+    nc = tc.nc
+    with ExitStack() as ctx:
+        keep = ctx.enter_context(tc.tile_pool(name="keep", bufs=1))
+        psum = ctx.enter_context(tc.psum_pool(name="psum", bufs=1))
+
+        reuse = ctx.enter_context(tc.tile_pool(name="reuse", bufs=1))
+
+        def tile(name, shape, dtype):
+            return keep.tile(shape, dtype, name=name, align_bytes=64)
+
+        def placed(name, shape, dtype, offset):
+            return reuse.tile(shape, dtype, name=name, align_bytes=64, offset=offset)
+
+        offs_sb = tile("offs_sb", [P, S // 16], U16)
+        a1_sb = tile("a1_sb", [P, S // 16], U16)
+        a2_sb = tile("a2_sb", [P, S // 16], U16)
+        row = 4 * U
+        scale_table = placed("scale_table", [P, T], U8, row - T // 2)
+        word_table = placed("word_table", [P, T], I32, 4 * row)
+        w1_raw = placed("w1_raw", [P, PACK, H], F32, 2 * row)
+        w2_raw = placed("w2_raw", [P, PACK, N], F32, 4 * row)
+        gn_sb = tile("gn_sb", [P, PACK], F32)
+        mem_sb = [placed("mem%d" % t, [P, U], F32, t * row) for t in range(PACK)]
+        picked_scales = tile("picked_scales", [P, S], U8)
+        x_plane = tile("x_plane", [P, S], U8)
+
+        nc.gpsimd.memset(x_plane[:].bitcast(I32), 0)
+        warm = tile("warm", [P, 2], F32)
+        nc.vector.memset(warm[:, 0:1], 0.0)
+
+        scale_rows = x_scales[0].bitcast(I32).rearrange("(r i) c -> r i c", i=2)
+        for i in range(2):
+            nc.sync.dma_start(
+                scale_table[i:P:2, :].bitcast(I32),
+                scale_rows[:, i : i + 1, :].to_broadcast([8, 8, T // 4]),
+            )
+        nc.sync.dma_start(offs_sb[:], offs)
+        nc.scalar.activation(warm[:, 1:2], warm[:, 0:1], SIGMOID)
+        nc.sync.dma_start(w1_raw[:], w1.rearrange("(p j) c -> p j c", j=PACK))
+        nc.sync.dma_start(word_table[:], x_words[0].rearrange("p c r -> p (c r)").bitcast(I32))
+        mem_rows = mem.rearrange("(p t) u -> p t u", t=PACK)
+
+        nc.vector.tensor_copy(picked_scales[:], scale_table[:].indirect(offs_sb[:]))
+        nc.scalar.dma_start(
+            x_plane[0:MOVED, :].bitcast(I32), picked_scales[STRADDLE : STRADDLE + MOVED, :].bitcast(I32)
+        )
+
+        nc.sync.dma_start(a1_sb[:], a1)
+        nc.sync.dma_start(mem_sb[0][:], mem_rows[:, 0, :])
+        nc.sync.dma_start(mem_sb[1][:], mem_rows[:, 1, :])
+        nc.sync.dma_start(a2_sb[:], a2)
+        nc.sync.dma_start(gn_sb[:], gn.rearrange("(p t) o -> p (t o)", t=PACK))
+
+        w1_grouped = tile("w1_grouped", [P, PACK * H], BF16)
+        w1_codes = tile("w1_codes", [P, H], U32)
+        w1_plane = tile("w1_plane", [P, H], U8)
+        nc.vector.tensor_copy(
+            w1_grouped[:].rearrange("p (t m j) -> p m j t", t=PACK, j=PACK),
+            w1_raw[:].rearrange("p j (m t) -> p m j t", t=PACK),
+        )
+        nc.sync.dma_start(mem_sb[2][:], mem_rows[:, 2, :])
+        nc.sync.dma_start(mem_sb[3][:], mem_rows[:, 3, :])
+        nc.vector.quantize_mx(w1_codes[:].bitcast(FP8X4), w1_plane[:], w1_grouped[:])
+
+        w2_grouped = tile("w2_grouped", [P, PACK * N], BF16)
+        w2_codes = tile("w2_codes", [P, N], U32)
+        w2_plane = tile("w2_plane", [P, N], U8)
+
+        def group_w2(b):
+            cols = slice(b * P, (b + 1) * P)
+            nc.scalar.copy(
+                w2_grouped[:, b * P * PACK : (b + 1) * P * PACK].rearrange("p (c i j) -> p c j i", i=4, j=PACK),
+                w2_raw[:, :, cols].rearrange("p j (c i) -> p c j i", i=4),
+            )
+
+        x_codes = {}
+        state = {}
+        z_planes = {}
+
+        def pick_words(c):
+            j0, n = CHUNKS[c]
+            x_codes[c] = tile("x_codes%d" % c, [P, n], U32)
+            nc.vector.tensor_copy(
+                x_codes[c][:], word_table[:].bitcast(U32).indirect(offs_sb[:, j0 // 16 : (j0 + n) // 16])
+            )
+            z_planes[c] = tile("z_planes%d" % c, [P, PACK, n], BF16)
+
+        def project(c, pair):
+            j0, n = CHUNKS[c]
+            y = psum.tile([P, 2, n], F32, name="y%d_%d" % (c, pair))
+            for i in range(2):
+                t = 2 * pair + i
+                nc.tensor.matmul_mx(
+                    y[:, i, :],
+                    lhsT=w1_codes[:, t * P : (t + 1) * P].bitcast(FP8X4),
+                    lhsT_scale=w1_plane[:, t * P : (t + 1) * P],
+                    rhs=x_codes[c][:].bitcast(FP8X4),
+                    rhs_scale=x_plane[:, j0 : j0 + n],
+                    start=True,
+                    stop=True,
+                )
+            gate = tile("gate1_%d_%d" % (c, pair), [P, 2, n], F32)
+            nc.scalar.activation(gate[:], y[:], SIGMOID)
+            state[c, pair] = (y, gate)
+
+        def hop1(c, pair):
+            j0, n = CHUNKS[c]
+            y, gate = state[c, pair]
+            read = tile("read1_%d_%d" % (c, pair), [P, 2, n], F32)
+            for i in range(2):
+                nc.vector.tensor_tensor(
+                    read[:, i, :],
+                    mem_sb[2 * pair + i][:].indirect(a1_sb[:, j0 // 16 : (j0 + n) // 16]),
+                    gate[:, i, :],
+                    MULT,
+                )
+            h = tile("h_%d_%d" % (c, pair), [P, 2, n], F32)
+            nc.vector.tensor_tensor(h[:], y[:], read[:], ADD)
+            gate2 = tile("gate2_%d_%d" % (c, pair), [P, 2, n], F32)
+            nc.scalar.activation(gate2[:], h[:], SIGMOID)
+            gained = tile("gained_%d_%d" % (c, pair), [P, 2, n], F32)
+            for i in range(2):
+                t = 2 * pair + i
+                nc.scalar.activation(gained[:, i, :], gate2[:, i, :], COPY, scale=gn_sb[:, t : t + 1])
+            state[c, pair] = (h, gained)
+
+        def hop2(c, pair):
+            j0, n = CHUNKS[c]
+            h, gained = state[c, pair]
+            read = tile("read2_%d_%d" % (c, pair), [P, 2, n], F32)
+            for i in range(2):
+                nc.vector.tensor_tensor(
+                    read[:, i, :],
+                    mem_sb[2 * pair + i][:].indirect(a2_sb[:, j0 // 16 : (j0 + n) // 16]),
+                    gained[:, i, :],
+                    MULT,
+                )
+            for i in range(2):
+                t = 2 * pair + i
+                nc.vector.scalar_tensor_tensor(
+                    z_planes[c][:, t, :], h[:, i, :], gn_sb[:, t : t + 1], read[:, i, :], MULT, ADD
+                )
+
+        def group_z(c, copy):
+            j0, n = CHUNKS[c]
+            grouped = tile("z_grouped%d" % c, [P, PACK * n], BF16)
+            copy(
+                grouped[:].rearrange("p (c i t) -> p c t i", i=4, t=PACK),
+                z_planes[c][:].rearrange("p t (c i) -> p c t i", i=4),
+            )
+            state[c] = grouped
+
+        def answer(c, copies):
+            j0, n = CHUNKS[c]
+            z_codes = tile("z_codes%d" % c, [P, n], U32)
+            z_plane = tile("z_plane%d" % c, [P, n], U8)
+            nc.vector.quantize_mx(z_codes[:].bitcast(FP8X4), z_plane[:], state[c][:])
+            for pair in range(2):
+                acc = psum.tile([P, 2, n], F32, name="acc%d_%d" % (c, pair))
+                for i in range(2):
+                    b = 2 * pair + i
+                    nc.tensor.matmul_mx(
+                        acc[:, i, :],
+                        lhsT=w2_codes[:, b * P : (b + 1) * P].bitcast(FP8X4),
+                        lhsT_scale=w2_plane[:, b * P : (b + 1) * P],
+                        rhs=z_codes[:].bitcast(FP8X4),
+                        rhs_scale=z_plane[:],
+                        start=True,
+                        stop=True,
+                    )
+                result = tile("result%d_%d" % (c, pair), [P, 2, n], F32)
+                copies[pair](result[:], acc[:])
+                nc.sync.dma_start(
+                    out[2 * pair * P : 2 * (pair + 1) * P, j0 : j0 + n].rearrange("(b p) j -> p b j", p=P),
+                    result[:],
+                )
+
+        pick_words(0)
+        project(0, 0)
+        project(0, 1)
+        pick_words(1)
+        nc.sync.dma_start(w2_raw[:], w2.rearrange("(p j) c -> p j c", j=PACK))
+        hop1(0, 0)
+        project(1, 0)
+        project(1, 1)
+        hop1(0, 1)
+        hop2(0, 0)
+        for b in range(PACK):
+            group_w2(b)
+        hop1(1, 0)
+        hop2(0, 1)
+        nc.vector.quantize_mx(w2_codes[:].bitcast(FP8X4), w2_plane[:], w2_grouped[:])
+        group_z(0, nc.scalar.copy)
+        hop1(1, 1)
+        hop2(1, 0)
+        answer(0, (nc.scalar.copy, nc.scalar.copy))
+        hop2(1, 1)
+        group_z(1, nc.vector.tensor_copy)
+        answer(1, (nc.scalar.copy, nc.vector.tensor_copy))

@@ -18,7 +18,8 @@ P = 128
 PACK = 4
 T, S, H, N, U = 2048, 512, 512, 512, 1024
 FLOPS = 2 * 512 * H * S + 2 * H * N * S
-CHUNKS = ((0, 256), (256, 256))
+CHUNKS = ((0, 256), (256, 128), (384, 128))
+EARLY = 2
 STRADDLE = 14
 MOVED = 112
 
@@ -43,9 +44,9 @@ def tile_picked_memhop2_none_p_kernel(
         a1_sb = tile("a1_sb", [P, S // 16], U16)
         a2_sb = tile("a2_sb", [P, S // 16], U16)
         row = 4 * U
-        scale_table = placed("scale_table", [P, T], U8, row - T // 2)
-        word_table = placed("word_table", [P, T], I32, 4 * row)
-        w1_raw = placed("w1_raw", [P, PACK, H], F32, 2 * row)
+        scale_table = placed("scale_table", [P, T], U8, 3 * row - T // 2)
+        word_table = tile("word_table", [P, T], I32)
+        w1_raw = placed("w1_raw", [P, PACK, H], F32, 4 * row)
         w2_raw = placed("w2_raw", [P, PACK, N], F32, 4 * row)
         gn_sb = tile("gn_sb", [P, PACK], F32)
         mem_sb = [placed("mem%d" % t, [P, U], F32, t * row) for t in range(PACK)]
@@ -63,31 +64,32 @@ def tile_picked_memhop2_none_p_kernel(
                 scale_rows[:, i : i + 1, :].to_broadcast([8, 8, T // 4]),
             )
         nc.sync.dma_start(offs_sb[:], offs)
+        mem_rows = mem.rearrange("(p t) u -> p t u", t=PACK)
+        nc.sync.dma_start(mem_sb[0][:], mem_rows[:, 0, :])
+        nc.sync.dma_start(a1_sb[:], a1)
+        nc.sync.dma_start(a2_sb[:], a2)
         nc.scalar.activation(warm[:, 1:2], warm[:, 0:1], SIGMOID)
         nc.sync.dma_start(w1_raw[:], w1.rearrange("(p j) c -> p j c", j=PACK))
         nc.sync.dma_start(word_table[:], x_words[0].rearrange("p c r -> p (c r)").bitcast(I32))
-        mem_rows = mem.rearrange("(p t) u -> p t u", t=PACK)
+        nc.sync.dma_start(mem_sb[1][:], mem_rows[:, 1, :])
+        nc.sync.dma_start(gn_sb[:], gn.rearrange("(p t) o -> p (t o)", t=PACK))
 
         nc.vector.tensor_copy(picked_scales[:], scale_table[:].indirect(offs_sb[:]))
         nc.scalar.dma_start(
             x_plane[0:MOVED, :].bitcast(I32), picked_scales[STRADDLE : STRADDLE + MOVED, :].bitcast(I32)
         )
 
-        nc.sync.dma_start(a1_sb[:], a1)
-        nc.sync.dma_start(mem_sb[0][:], mem_rows[:, 0, :])
-        nc.sync.dma_start(mem_sb[1][:], mem_rows[:, 1, :])
-        nc.sync.dma_start(a2_sb[:], a2)
-        nc.sync.dma_start(gn_sb[:], gn.rearrange("(p t) o -> p (t o)", t=PACK))
+        nc.sync.dma_start(mem_sb[2][:], mem_rows[:, 2, :])
+        nc.sync.dma_start(mem_sb[3][:], mem_rows[:, 3, :])
 
         w1_grouped = tile("w1_grouped", [P, PACK * H], BF16)
         w1_codes = tile("w1_codes", [P, H], U32)
         w1_plane = tile("w1_plane", [P, H], U8)
-        nc.vector.tensor_copy(
+        nc.scalar.copy(
             w1_grouped[:].rearrange("p (t m j) -> p m j t", t=PACK, j=PACK),
             w1_raw[:].rearrange("p j (m t) -> p m j t", t=PACK),
         )
-        nc.sync.dma_start(mem_sb[2][:], mem_rows[:, 2, :])
-        nc.sync.dma_start(mem_sb[3][:], mem_rows[:, 3, :])
+        nc.sync.dma_start(w2_raw[:], w2.rearrange("(p j) c -> p j c", j=PACK))
         nc.vector.quantize_mx(w1_codes[:].bitcast(FP8X4), w1_plane[:], w1_grouped[:])
 
         w2_grouped = tile("w2_grouped", [P, PACK * N], BF16)
@@ -101,92 +103,85 @@ def tile_picked_memhop2_none_p_kernel(
                 w2_raw[:, :, cols].rearrange("p j (c i) -> p c j i", i=4),
             )
 
-        x_codes = {}
         state = {}
-        z_planes = {}
+        slots = {}
+        x_codes = tile("x_codes", [P, S], U32)
+        z_planes = tile("z_planes", [P, PACK, S], BF16)
 
-        def pick_words(c):
-            j0, n = CHUNKS[c]
-            x_codes[c] = tile("x_codes%d" % c, [P, n], U32)
-            nc.vector.tensor_copy(
-                x_codes[c][:], word_table[:].bitcast(U32).indirect(offs_sb[:, j0 // 16 : (j0 + n) // 16])
+        def fetch(t):
+            for hop, lists in enumerate((a1_sb, a2_sb)):
+                slots[hop, t] = tile("slot%d_%d" % (hop, t), [P, S], F32)
+                nc.vector.tensor_copy(slots[hop, t][:], mem_sb[t][:].indirect(lists[:]))
+
+        def project(t):
+            y = psum.tile([P, S], F32, name="y%d" % t, tag="bank%d" % t)
+            nc.tensor.matmul_mx(
+                y[:],
+                lhsT=w1_codes[:, t * P : (t + 1) * P].bitcast(FP8X4),
+                lhsT_scale=w1_plane[:, t * P : (t + 1) * P],
+                rhs=x_codes[:].bitcast(FP8X4),
+                rhs_scale=x_plane[:],
+                start=True,
+                stop=True,
             )
-            z_planes[c] = tile("z_planes%d" % c, [P, PACK, n], BF16)
-
-        def project(c, pair):
-            j0, n = CHUNKS[c]
-            y = psum.tile([P, 2, n], F32, name="y%d_%d" % (c, pair))
-            for i in range(2):
-                t = 2 * pair + i
-                nc.tensor.matmul_mx(
-                    y[:, i, :],
-                    lhsT=w1_codes[:, t * P : (t + 1) * P].bitcast(FP8X4),
-                    lhsT_scale=w1_plane[:, t * P : (t + 1) * P],
-                    rhs=x_codes[c][:].bitcast(FP8X4),
-                    rhs_scale=x_plane[:, j0 : j0 + n],
-                    start=True,
-                    stop=True,
-                )
-            gate = tile("gate1_%d_%d" % (c, pair), [P, 2, n], F32)
+            gate = tile("gate1_%d" % t, [P, S], F32)
             nc.scalar.activation(gate[:], y[:], SIGMOID)
-            state[c, pair] = (y, gate)
+            state["y", t] = (y, gate)
 
-        def hop1(c, pair):
-            j0, n = CHUNKS[c]
-            y, gate = state[c, pair]
-            read = tile("read1_%d_%d" % (c, pair), [P, 2, n], F32)
-            for i in range(2):
-                nc.vector.tensor_tensor(
-                    read[:, i, :],
-                    mem_sb[2 * pair + i][:].indirect(a1_sb[:, j0 // 16 : (j0 + n) // 16]),
-                    gate[:, i, :],
-                    MULT,
-                )
-            h = tile("h_%d_%d" % (c, pair), [P, 2, n], F32)
-            nc.vector.tensor_tensor(h[:], y[:], read[:], ADD)
-            gate2 = tile("gate2_%d_%d" % (c, pair), [P, 2, n], F32)
+        def gate1(t):
+            y, gate = state["y", t]
+            state["read1", t] = tile("read1_%d" % t, [P, S], F32)
+            slot = slots[0, t][:] if t < EARLY else mem_sb[t][:].indirect(a1_sb[:])
+            nc.vector.tensor_tensor(state["read1", t][:], slot, gate[:], MULT)
+
+        def hop1(t):
+            y, gate = state["y", t]
+            h = tile("h_%d" % t, [P, S], F32)
+            nc.vector.tensor_tensor(h[:], y[:], state["read1", t][:], ADD)
+            gate2 = tile("gate2_%d" % t, [P, S], F32)
             nc.scalar.activation(gate2[:], h[:], SIGMOID)
-            gained = tile("gained_%d_%d" % (c, pair), [P, 2, n], F32)
-            for i in range(2):
-                t = 2 * pair + i
-                nc.scalar.activation(gained[:, i, :], gate2[:, i, :], COPY, scale=gn_sb[:, t : t + 1])
-            state[c, pair] = (h, gained)
+            if t >= EARLY:
+                gained = tile("gained_%d" % t, [P, S], F32)
+                nc.scalar.activation(gained[:], gate2[:], COPY, scale=gn_sb[:, t : t + 1])
+                gate2 = gained
+            state["h", t] = (h, gate2)
 
-        def hop2(c, pair):
-            j0, n = CHUNKS[c]
-            h, gained = state[c, pair]
-            read = tile("read2_%d_%d" % (c, pair), [P, 2, n], F32)
-            for i in range(2):
-                nc.vector.tensor_tensor(
-                    read[:, i, :],
-                    mem_sb[2 * pair + i][:].indirect(a2_sb[:, j0 // 16 : (j0 + n) // 16]),
-                    gained[:, i, :],
-                    MULT,
-                )
-            for i in range(2):
-                t = 2 * pair + i
+        def gate2(t, j0, n):
+            h, gate = state["h", t]
+            read = tile("read2_%d_%d" % (t, j0), [P, n], F32)
+            state["read2", t, j0] = read
+            if t < EARLY:
                 nc.vector.scalar_tensor_tensor(
-                    z_planes[c][:, t, :], h[:, i, :], gn_sb[:, t : t + 1], read[:, i, :], MULT, ADD
+                    read[:], gate[:, j0 : j0 + n], gn_sb[:, t : t + 1], slots[1, t][:, j0 : j0 + n], MULT, MULT
+                )
+            else:
+                nc.vector.tensor_tensor(
+                    read[:], mem_sb[t][:].indirect(a2_sb[:, j0 // 16 : (j0 + n) // 16]), gate[:, j0 : j0 + n], MULT
                 )
 
-        def group_z(c, copy):
-            j0, n = CHUNKS[c]
-            grouped = tile("z_grouped%d" % c, [P, PACK * n], BF16)
+        def hop2(t, j0, n):
+            h, gate = state["h", t]
+            nc.vector.scalar_tensor_tensor(
+                z_planes[:, t, j0 : j0 + n], h[:, j0 : j0 + n], gn_sb[:, t : t + 1], state["read2", t, j0][:], MULT, ADD
+            )
+
+        def group_z(j0, n, copy):
+            grouped = tile("z_grouped%d" % j0, [P, PACK * n], BF16)
             copy(
                 grouped[:].rearrange("p (c i t) -> p c t i", i=4, t=PACK),
-                z_planes[c][:].rearrange("p t (c i) -> p c t i", i=4),
+                z_planes[:, :, j0 : j0 + n].rearrange("p t (c i) -> p c t i", i=4),
             )
-            state[c] = grouped
+            state["z", j0] = grouped
 
-        def answer(c, copies):
-            j0, n = CHUNKS[c]
-            z_codes = tile("z_codes%d" % c, [P, n], U32)
-            z_plane = tile("z_plane%d" % c, [P, n], U8)
-            nc.vector.quantize_mx(z_codes[:].bitcast(FP8X4), z_plane[:], state[c][:])
-            for pair in range(2):
-                acc = psum.tile([P, 2, n], F32, name="acc%d_%d" % (c, pair))
-                for i in range(2):
-                    b = 2 * pair + i
+        def answer(j0, n, banks, copies):
+            z_codes = tile("z_codes%d" % j0, [P, n], U32)
+            z_plane = tile("z_plane%d" % j0, [P, n], U8)
+            nc.vector.quantize_mx(z_codes[:].bitcast(FP8X4), z_plane[:], state["z", j0][:])
+            share = PACK // len(banks)
+            for g, (bank, copy) in enumerate(zip(banks, copies)):
+                acc = psum.tile([P, share, n], F32, name="acc%d_%d" % (j0, g), tag="bank%d" % bank)
+                for i in range(share):
+                    b = share * g + i
                     nc.tensor.matmul_mx(
                         acc[:, i, :],
                         lhsT=w2_codes[:, b * P : (b + 1) * P].bitcast(FP8X4),
@@ -196,32 +191,41 @@ def tile_picked_memhop2_none_p_kernel(
                         start=True,
                         stop=True,
                     )
-                result = tile("result%d_%d" % (c, pair), [P, 2, n], F32)
-                copies[pair](result[:], acc[:])
+                result = tile("result%d_%d" % (j0, g), [P, share, n], F32)
+                copy(result[:], acc[:])
                 nc.sync.dma_start(
-                    out[2 * pair * P : 2 * (pair + 1) * P, j0 : j0 + n].rearrange("(b p) j -> p b j", p=P),
+                    out[share * g * P : share * (g + 1) * P, j0 : j0 + n].rearrange("(b p) j -> p b j", p=P),
                     result[:],
                 )
 
-        pick_words(0)
-        project(0, 0)
-        project(0, 1)
-        pick_words(1)
-        nc.sync.dma_start(w2_raw[:], w2.rearrange("(p j) c -> p j c", j=PACK))
-        hop1(0, 0)
-        project(1, 0)
-        project(1, 1)
-        hop1(0, 1)
-        hop2(0, 0)
+        fetch(0)
+        nc.vector.tensor_copy(x_codes[:], word_table[:].bitcast(U32).indirect(offs_sb[:]))
+        for t in range(PACK):
+            project(t)
+        fetch(1)
+        gate1(0)
+        gate1(1)
+        hop1(0)
+        hop1(1)
+        gate1(2)
+        gate1(3)
+        hop1(2)
+        hop1(3)
+        for t in range(EARLY):
+            gate2(t, 0, S)
+        for t in range(EARLY):
+            hop2(t, 0, S)
         for b in range(PACK):
             group_w2(b)
-        hop1(1, 0)
-        hop2(0, 1)
         nc.vector.quantize_mx(w2_codes[:].bitcast(FP8X4), w2_plane[:], w2_grouped[:])
-        group_z(0, nc.scalar.copy)
-        hop1(1, 1)
-        hop2(1, 0)
-        answer(0, (nc.scalar.copy, nc.scalar.copy))
-        hop2(1, 1)
-        group_z(1, nc.vector.tensor_copy)
-        answer(1, (nc.scalar.copy, nc.vector.tensor_copy))
+        on_scalar, on_vector = nc.scalar.copy, nc.vector.tensor_copy
+        ways_out = (((4, 5), (on_scalar, on_scalar)), ((6,), (on_scalar,)), ((7, 0), (on_scalar, on_vector)))
+        for c, (j0, n) in enumerate(CHUNKS):
+            for t in range(EARLY, PACK):
+                gate2(t, j0, n)
+            for t in range(EARLY, PACK):
+                hop2(t, j0, n)
+            group_z(j0, n, on_vector if c == len(CHUNKS) - 1 else on_scalar)
+            if c:
+                answer(*CHUNKS[c - 1], *ways_out[c - 1])
+        answer(*CHUNKS[-1], *ways_out[-1])

@@ -16,12 +16,16 @@ COPY = mybir.ActivationFunctionType.Copy
 
 P = 128
 PACK = 4
-T, S, H, N, U = 2048, 512, 512, 512, 1024
-FLOPS = 2 * 512 * H * S + 2 * H * N * S
-CHUNKS = ((0, 256), (256, 128), (384, 128))
-EARLY = 2
-STRADDLE = 14
-MOVED = 112
+GROUP = 16
+QUADRANT = 32
+BLOCK = 8
+K, T, S, H, N, U = 512, 2048, 512, 512, 512, 1024
+FLOPS = 2 * K * H * S + 2 * H * N * S
+
+HALF = S // 2
+CHUNKS = ((0, HALF), (HALF, P), (HALF + P, P))
+WIDE = 2
+ROW = 4 * U
 
 
 def tile_picked_memhop2_none_p_kernel(
@@ -31,7 +35,6 @@ def tile_picked_memhop2_none_p_kernel(
     with ExitStack() as ctx:
         keep = ctx.enter_context(tc.tile_pool(name="keep", bufs=1))
         psum = ctx.enter_context(tc.psum_pool(name="psum", bufs=1))
-
         reuse = ctx.enter_context(tc.tile_pool(name="reuse", bufs=1))
 
         def tile(name, shape, dtype):
@@ -40,144 +43,123 @@ def tile_picked_memhop2_none_p_kernel(
         def placed(name, shape, dtype, offset):
             return reuse.tile(shape, dtype, name=name, align_bytes=64, offset=offset)
 
-        offs_sb = tile("offs_sb", [P, S // 16], U16)
-        a1_sb = tile("a1_sb", [P, S // 16], U16)
-        a2_sb = tile("a2_sb", [P, S // 16], U16)
-        row = 4 * U
-        scale_table = placed("scale_table", [P, T], U8, 3 * row - T // 2)
-        word_table = tile("word_table", [P, T], I32)
-        w1_raw = placed("w1_raw", [P, PACK, H], F32, 4 * row)
-        w2_raw = placed("w2_raw", [P, PACK, N], F32, 4 * row)
+        def entries(lists, j0, n):
+            return lists[:, j0 // GROUP : (j0 + n) // GROUP]
+
+        offs_sb = tile("offs_sb", [P, S // GROUP], U16)
+        a1_sb = tile("a1_sb", [P, S // GROUP], U16)
+        a2_sb = tile("a2_sb", [P, S // GROUP], U16)
+        scale_table = placed("scale_table", [P, T], U8, ROW - T // 2)
+        word_table = placed("word_table", [P, T], I32, 4 * ROW)
+        w1_raw = placed("w1_raw", [P, PACK, H], F32, 2 * ROW)
+        w2_raw = placed("w2_raw", [P, PACK, N], F32, 4 * ROW)
         gn_sb = tile("gn_sb", [P, PACK], F32)
-        mem_sb = [placed("mem%d" % t, [P, U], F32, t * row) for t in range(PACK)]
+        mem_sb = [placed("mem%d" % t, [P, U], F32, t * ROW) for t in range(PACK)]
         picked_scales = tile("picked_scales", [P, S], U8)
-        x_plane = tile("x_plane", [P, S], U8)
+        x_scale_rows = tile("x_scale_rows", [P, S], U8)
+        first_grouped_at = 6 * ROW
+        gated_ring_at = 7 * ROW
 
-        nc.gpsimd.memset(x_plane[:].bitcast(I32), 0)
-        warm = tile("warm", [P, 2], F32)
-        nc.vector.memset(warm[:, 0:1], 0.0)
+        nc.vector.memset(x_scale_rows[:].bitcast(I32), 0)
 
-        scale_rows = x_scales[0].bitcast(I32).rearrange("(r i) c -> r i c", i=2)
-        for i in range(2):
-            nc.sync.dma_start(
-                scale_table[i:P:2, :].bitcast(I32),
-                scale_rows[:, i : i + 1, :].to_broadcast([8, 8, T // 4]),
-            )
+        nc.sync.dma_start(
+            scale_table[:].bitcast(I32),
+            x_scales[0].bitcast(I32).unsqueeze(1).to_broadcast([P // BLOCK, BLOCK, T // 4]),
+        )
         nc.sync.dma_start(offs_sb[:], offs)
-        mem_rows = mem.rearrange("(p t) u -> p t u", t=PACK)
-        nc.sync.dma_start(mem_sb[0][:], mem_rows[:, 0, :])
         nc.sync.dma_start(a1_sb[:], a1)
         nc.sync.dma_start(a2_sb[:], a2)
-        nc.scalar.activation(warm[:, 1:2], warm[:, 0:1], SIGMOID)
+        nc.sync.dma_start(gn_sb[:], gn.rearrange("(p t) o -> p (t o)", t=PACK))
         nc.sync.dma_start(w1_raw[:], w1.rearrange("(p j) c -> p j c", j=PACK))
         nc.sync.dma_start(word_table[:], x_words[0].rearrange("p c r -> p (c r)").bitcast(I32))
-        nc.sync.dma_start(mem_sb[1][:], mem_rows[:, 1, :])
-        nc.sync.dma_start(gn_sb[:], gn.rearrange("(p t) o -> p (t o)", t=PACK))
 
         nc.vector.tensor_copy(picked_scales[:], scale_table[:].indirect(offs_sb[:]))
-        nc.scalar.dma_start(
-            x_plane[0:MOVED, :].bitcast(I32), picked_scales[STRADDLE : STRADDLE + MOVED, :].bitcast(I32)
-        )
-
-        nc.sync.dma_start(mem_sb[2][:], mem_rows[:, 2, :])
-        nc.sync.dma_start(mem_sb[3][:], mem_rows[:, 3, :])
+        for i in range(QUADRANT // BLOCK):
+            nc.sync.dma_start(
+                x_scale_rows[i:P:QUADRANT, :].bitcast(I32), picked_scales[BLOCK * i : P : QUADRANT, :].bitcast(I32)
+            )
+        mem_rows = mem.rearrange("(p t) u -> p t u", t=PACK)
+        nc.sync.dma_start(mem_sb[0][:], mem_rows[:, 0, :])
+        nc.sync.dma_start(mem_sb[1][:], mem_rows[:, 1, :])
 
         w1_grouped = tile("w1_grouped", [P, PACK * H], BF16)
         w1_codes = tile("w1_codes", [P, H], U32)
-        w1_plane = tile("w1_plane", [P, H], U8)
-        nc.scalar.copy(
+        w1_scale_rows = tile("w1_scale_rows", [P, H], U8)
+        nc.vector.tensor_copy(
             w1_grouped[:].rearrange("p (t m j) -> p m j t", t=PACK, j=PACK),
             w1_raw[:].rearrange("p j (m t) -> p m j t", t=PACK),
         )
-        nc.sync.dma_start(w2_raw[:], w2.rearrange("(p j) c -> p j c", j=PACK))
-        nc.vector.quantize_mx(w1_codes[:].bitcast(FP8X4), w1_plane[:], w1_grouped[:])
+        nc.sync.dma_start(mem_sb[2][:], mem_rows[:, 2, :])
+        nc.sync.dma_start(mem_sb[3][:], mem_rows[:, 3, :])
+        nc.vector.quantize_mx(w1_codes[:].bitcast(FP8X4), w1_scale_rows[:], w1_grouped[:])
 
         w2_grouped = tile("w2_grouped", [P, PACK * N], BF16)
         w2_codes = tile("w2_codes", [P, N], U32)
-        w2_plane = tile("w2_plane", [P, N], U8)
+        w2_scale_rows = tile("w2_scale_rows", [P, N], U8)
+        x_codes = tile("x_codes", [P, S], U32)
+        z_quarters = tile("z_quarters", [P, PACK, S], BF16)
+        y, y_gate, gated1, h, h_gate = ([None] * PACK for kind in range(5))
+        gated2, z_grouped = {}, {}
 
-        def group_w2(b):
-            cols = slice(b * P, (b + 1) * P)
-            nc.scalar.copy(
-                w2_grouped[:, b * P * PACK : (b + 1) * P * PACK].rearrange("p (c i j) -> p c j i", i=4, j=PACK),
-                w2_raw[:, :, cols].rearrange("p j (c i) -> p c j i", i=4),
+        def interleave(copy, grouped, quarters):
+            copy(
+                grouped.rearrange("p (c i t) -> p c t i", i=4, t=PACK),
+                quarters.rearrange("p t (c i) -> p c t i", i=4),
             )
 
-        state = {}
-        slots = {}
-        x_codes = tile("x_codes", [P, S], U32)
-        z_planes = tile("z_planes", [P, PACK, S], BF16)
-
-        def fetch(t):
-            for hop, lists in enumerate((a1_sb, a2_sb)):
-                slots[hop, t] = tile("slot%d_%d" % (hop, t), [P, S], F32)
-                nc.vector.tensor_copy(slots[hop, t][:], mem_sb[t][:].indirect(lists[:]))
-
         def project(t):
-            y = psum.tile([P, S], F32, name="y%d" % t, tag="bank%d" % t)
+            y[t] = psum.tile([P, S], F32, name="y%d" % t, tag="bank%d" % t)
             nc.tensor.matmul_mx(
-                y[:],
+                y[t][:],
                 lhsT=w1_codes[:, t * P : (t + 1) * P].bitcast(FP8X4),
-                lhsT_scale=w1_plane[:, t * P : (t + 1) * P],
+                lhsT_scale=w1_scale_rows[:, t * P : (t + 1) * P],
                 rhs=x_codes[:].bitcast(FP8X4),
-                rhs_scale=x_plane[:],
+                rhs_scale=x_scale_rows[:],
                 start=True,
                 stop=True,
             )
-            gate = tile("gate1_%d" % t, [P, S], F32)
-            nc.scalar.activation(gate[:], y[:], SIGMOID)
-            state["y", t] = (y, gate)
+            y_gate[t] = tile("y_gate%d" % t, [P, S], F32)
+            nc.scalar.activation(y_gate[t][:], y[t][:], SIGMOID)
 
-        def gate1(t):
-            y, gate = state["y", t]
-            state["read1", t] = tile("read1_%d" % t, [P, S], F32)
-            slot = slots[0, t][:] if t < EARLY else mem_sb[t][:].indirect(a1_sb[:])
-            nc.vector.tensor_tensor(state["read1", t][:], slot, gate[:], MULT)
+        def gate_first_slots(t, slots):
+            gated1[t] = tile("gated1_%d" % t, [P, S], F32)
+            nc.vector.tensor_tensor(gated1[t][:], slots, y_gate[t][:], MULT)
 
-        def hop1(t):
-            y, gate = state["y", t]
-            h = tile("h_%d" % t, [P, S], F32)
-            nc.vector.tensor_tensor(h[:], y[:], state["read1", t][:], ADD)
-            gate2 = tile("gate2_%d" % t, [P, S], F32)
-            nc.scalar.activation(gate2[:], h[:], SIGMOID)
-            if t >= EARLY:
-                gained = tile("gained_%d" % t, [P, S], F32)
-                nc.scalar.activation(gained[:], gate2[:], COPY, scale=gn_sb[:, t : t + 1])
-                gate2 = gained
-            state["h", t] = (h, gate2)
+        def close_first_hop(t):
+            h[t] = tile("h%d" % t, [P, S], F32)
+            nc.vector.tensor_tensor(h[t][:], y[t][:], gated1[t][:], ADD)
+            bare_gate = tile("bare_gate%d" % t, [P, S], F32)
+            nc.scalar.activation(bare_gate[:], h[t][:], SIGMOID)
+            h_gate[t] = tile("h_gate%d" % t, [P, S], F32)
+            nc.scalar.activation(h_gate[t][:], bare_gate[:], COPY, scale=gn_sb[:, t : t + 1])
 
-        def gate2(t, j0, n):
-            h, gate = state["h", t]
-            read = tile("read2_%d_%d" % (t, j0), [P, n], F32)
-            state["read2", t, j0] = read
-            if t < EARLY:
-                nc.vector.scalar_tensor_tensor(
-                    read[:], gate[:, j0 : j0 + n], gn_sb[:, t : t + 1], slots[1, t][:, j0 : j0 + n], MULT, MULT
-                )
-            else:
+        def second_hop(quarters, j0, n):
+            for t in quarters:
+                if j0 == CHUNKS[-1][0]:
+                    offset = first_grouped_at + (t - WIDE) * 4 * n
+                else:
+                    offset = gated_ring_at + (t + 2 * (j0 // HALF)) % PACK * 4 * HALF
+                gated2[t] = placed("gated2_%d_%d" % (t, j0), [P, n], F32, offset)
                 nc.vector.tensor_tensor(
-                    read[:], mem_sb[t][:].indirect(a2_sb[:, j0 // 16 : (j0 + n) // 16]), gate[:, j0 : j0 + n], MULT
+                    gated2[t][:], mem_sb[t][:].indirect(entries(a2_sb, j0, n)), h_gate[t][:, j0 : j0 + n], MULT
                 )
-
-        def hop2(t, j0, n):
-            h, gate = state["h", t]
-            nc.vector.scalar_tensor_tensor(
-                z_planes[:, t, j0 : j0 + n], h[:, j0 : j0 + n], gn_sb[:, t : t + 1], state["read2", t, j0][:], MULT, ADD
-            )
+            for t in quarters:
+                nc.vector.scalar_tensor_tensor(
+                    z_quarters[:, t, j0 : j0 + n], h[t][:, j0 : j0 + n], gn_sb[:, t : t + 1], gated2[t][:], MULT, ADD
+                )
 
         def group_z(j0, n, copy):
-            grouped = tile("z_grouped%d" % j0, [P, PACK * n], BF16)
-            copy(
-                grouped[:].rearrange("p (c i t) -> p c t i", i=4, t=PACK),
-                z_planes[:, :, j0 : j0 + n].rearrange("p t (c i) -> p c t i", i=4),
-            )
-            state["z", j0] = grouped
+            if j0 == 0:
+                z_grouped[j0] = placed("z_grouped%d" % j0, [P, PACK * n], BF16, first_grouped_at)
+            else:
+                z_grouped[j0] = tile("z_grouped%d" % j0, [P, PACK * n], BF16)
+            interleave(copy, z_grouped[j0][:], z_quarters[:, :, j0 : j0 + n])
 
         def answer(j0, n, banks, copies):
             z_codes = tile("z_codes%d" % j0, [P, n], U32)
-            z_plane = tile("z_plane%d" % j0, [P, n], U8)
-            nc.vector.quantize_mx(z_codes[:].bitcast(FP8X4), z_plane[:], state["z", j0][:])
-            share = PACK // len(banks)
+            z_scale_rows = tile("z_scale_rows%d" % j0, [P, n], U8)
+            nc.vector.quantize_mx(z_codes[:].bitcast(FP8X4), z_scale_rows[:], z_grouped[j0][:])
+            share = N // P // len(banks)
             for g, (bank, copy) in enumerate(zip(banks, copies)):
                 acc = psum.tile([P, share, n], F32, name="acc%d_%d" % (j0, g), tag="bank%d" % bank)
                 for i in range(share):
@@ -185,9 +167,9 @@ def tile_picked_memhop2_none_p_kernel(
                     nc.tensor.matmul_mx(
                         acc[:, i, :],
                         lhsT=w2_codes[:, b * P : (b + 1) * P].bitcast(FP8X4),
-                        lhsT_scale=w2_plane[:, b * P : (b + 1) * P],
+                        lhsT_scale=w2_scale_rows[:, b * P : (b + 1) * P],
                         rhs=z_codes[:].bitcast(FP8X4),
-                        rhs_scale=z_plane[:],
+                        rhs_scale=z_scale_rows[:],
                         start=True,
                         stop=True,
                     )
@@ -198,33 +180,31 @@ def tile_picked_memhop2_none_p_kernel(
                     result[:],
                 )
 
-        fetch(0)
         nc.vector.tensor_copy(x_codes[:], word_table[:].bitcast(U32).indirect(offs_sb[:]))
+        nc.sync.dma_start(w2_raw[:], w2.rearrange("(p j) c -> p j c", j=PACK))
         for t in range(PACK):
             project(t)
-        fetch(1)
-        gate1(0)
-        gate1(1)
-        hop1(0)
-        hop1(1)
-        gate1(2)
-        gate1(3)
-        hop1(2)
-        hop1(3)
-        for t in range(EARLY):
-            gate2(t, 0, S)
-        for t in range(EARLY):
-            hop2(t, 0, S)
-        for b in range(PACK):
-            group_w2(b)
-        nc.vector.quantize_mx(w2_codes[:].bitcast(FP8X4), w2_plane[:], w2_grouped[:])
+
+        first_slots = tile("first_slots", [P, S], F32)
+        nc.vector.tensor_copy(first_slots[:], mem_sb[0][:].indirect(a1_sb[:]))
+        for pair in ((0, 1), (2, 3)):
+            for t in pair:
+                gate_first_slots(t, mem_sb[t][:].indirect(a1_sb[:]) if t else first_slots[:])
+            for t in pair:
+                close_first_hop(t)
+
+        for b in range(N // P):
+            interleave(
+                nc.scalar.copy, w2_grouped[:, b * P * PACK : (b + 1) * P * PACK], w2_raw[:, :, b * P : (b + 1) * P]
+            )
+        nc.vector.quantize_mx(w2_codes[:].bitcast(FP8X4), w2_scale_rows[:], w2_grouped[:])
+
         on_scalar, on_vector = nc.scalar.copy, nc.vector.tensor_copy
         ways_out = (((4, 5), (on_scalar, on_scalar)), ((6,), (on_scalar,)), ((7, 0), (on_scalar, on_vector)))
         for c, (j0, n) in enumerate(CHUNKS):
-            for t in range(EARLY, PACK):
-                gate2(t, j0, n)
-            for t in range(EARLY, PACK):
-                hop2(t, j0, n)
+            if j0 % HALF == 0:
+                second_hop(range(WIDE), j0, HALF)
+            second_hop(range(WIDE, PACK), j0, n)
             group_z(j0, n, on_vector if c == len(CHUNKS) - 1 else on_scalar)
             if c:
                 answer(*CHUNKS[c - 1], *ways_out[c - 1])

@@ -23,8 +23,6 @@ K, T, S, H, N, U = 512, 2048, 512, 512, 512, 1024
 FLOPS = 2 * K * H * S + 2 * H * N * S
 
 HALF = S // 2
-CHUNKS = ((0, HALF), (HALF, P), (HALF + P, P))
-WIDE = 2
 ROW = 4 * U
 
 
@@ -50,39 +48,37 @@ def tile_picked_memhop2_none_p_kernel(
         a1_sb = tile("a1_sb", [P, S // GROUP], U16)
         a2_sb = tile("a2_sb", [P, S // GROUP], U16)
         scale_table = placed("scale_table", [P, T], U8, ROW - T // 2)
-        word_table = placed("word_table", [P, T], I32, 4 * ROW)
         w1_raw = placed("w1_raw", [P, PACK, H], F32, 2 * ROW)
-        w2_raw = placed("w2_raw", [P, PACK, N], F32, 4 * ROW)
+        word_table = placed("word_table", [P, T], I32, 4 * ROW)
+        mem_sb = [placed("mem%d" % t, [P, U], F32, row * ROW) for t, row in enumerate((0, 1, 2, 3))]
+        w2_raw = [placed("w2_raw%d" % g, [P, PACK, N // 2], F32, row * ROW) for g, row in enumerate((4, 5))]
+        w1_grouped = tile("w1_grouped", [P, PACK * H], BF16)
         gn_sb = tile("gn_sb", [P, PACK], F32)
-        mem_sb = [placed("mem%d" % t, [P, U], F32, t * ROW) for t in range(PACK)]
         picked_scales = tile("picked_scales", [P, S], U8)
         x_scale_rows = tile("x_scale_rows", [P, S], U8)
-        first_grouped_at = 6 * ROW
-        gated_ring_at = 7 * ROW
-
-        nc.vector.memset(x_scale_rows[:].bitcast(I32), 0)
 
         nc.sync.dma_start(
             scale_table[:].bitcast(I32),
             x_scales[0].bitcast(I32).unsqueeze(1).to_broadcast([P // BLOCK, BLOCK, T // 4]),
         )
         nc.sync.dma_start(offs_sb[:], offs)
+        nc.sync.dma_start(w1_raw[:], w1.rearrange("(p j) c -> p j c", j=PACK))
+        nc.sync.dma_start(word_table[:], x_words[0].rearrange("p c r -> p (c r)").bitcast(I32))
         nc.sync.dma_start(a1_sb[:], a1)
         nc.sync.dma_start(a2_sb[:], a2)
         nc.sync.dma_start(gn_sb[:], gn.rearrange("(p t) o -> p (t o)", t=PACK))
-        nc.sync.dma_start(w1_raw[:], w1.rearrange("(p j) c -> p j c", j=PACK))
-        nc.sync.dma_start(word_table[:], x_words[0].rearrange("p c r -> p (c r)").bitcast(I32))
 
         nc.vector.tensor_copy(picked_scales[:], scale_table[:].indirect(offs_sb[:]))
-        for i in range(QUADRANT // BLOCK):
+        nc.vector.tensor_copy(x_scale_rows[:].bitcast(I32), picked_scales[:].bitcast(I32))
+        for i in range(1, QUADRANT // BLOCK):
             nc.sync.dma_start(
                 x_scale_rows[i:P:QUADRANT, :].bitcast(I32), picked_scales[BLOCK * i : P : QUADRANT, :].bitcast(I32)
             )
         mem_rows = mem.rearrange("(p t) u -> p t u", t=PACK)
+        w2_rows = w2.rearrange("(p j) c -> p j c", j=PACK)
         nc.sync.dma_start(mem_sb[0][:], mem_rows[:, 0, :])
         nc.sync.dma_start(mem_sb[1][:], mem_rows[:, 1, :])
 
-        w1_grouped = tile("w1_grouped", [P, PACK * H], BF16)
         w1_codes = tile("w1_codes", [P, H], U32)
         w1_scale_rows = tile("w1_scale_rows", [P, H], U8)
         nc.vector.tensor_copy(
@@ -97,115 +93,187 @@ def tile_picked_memhop2_none_p_kernel(
         w2_codes = tile("w2_codes", [P, N], U32)
         w2_scale_rows = tile("w2_scale_rows", [P, N], U8)
         x_codes = tile("x_codes", [P, S], U32)
-        z_quarters = tile("z_quarters", [P, PACK, S], BF16)
-        y, y_gate, gated1, h, h_gate = ([None] * PACK for kind in range(5))
-        gated2, z_grouped = {}, {}
+        y, bare_gate = {}, [None] * PACK
+        y_gate = [tile("y_gate%d" % t, [P, S], F32) for t in range(PACK)]
+        gated1 = [tile("gated1_%d" % t, [P, S], F32) for t in range(PACK)]
+        h = [tile("h%d" % t, [P, S], F32) for t in range(PACK)]
+        h_gate = [[tile("h_gate%d_%d" % (g, t), [P, HALF], F32) for t in range(PACK)] for g in range(2)]
+        gained_h = [tile("gained_h%d" % g, [P, PACK, HALF], F32) for g in range(2)]
+        gated2 = [tile("gated2_%d" % g, [P, PACK, HALF], F32) for g in range(2)]
+        z_grouped, z_codes, z_scale_rows = {}, {}, {}
 
-        def interleave(copy, grouped, quarters):
-            copy(
-                grouped.rearrange("p (c i t) -> p c t i", i=4, t=PACK),
-                quarters.rearrange("p t (c i) -> p c t i", i=4),
-            )
+        def woven(grouped):
+            return grouped.rearrange("p (c i t) -> p c t i", i=4, t=PACK)
 
-        def project(t):
-            y[t] = psum.tile([P, S], F32, name="y%d" % t, tag="bank%d" % t)
+        def by_fours(quarters):
+            return quarters.rearrange("p t (c i) -> p c t i", i=4)
+
+        def project(t, j0, n, bank):
+            y[t, j0] = psum.tile([P, n], F32, name="y%d_%d" % (t, j0), tag="bank%d" % bank)
             nc.tensor.matmul_mx(
-                y[t][:],
+                y[t, j0][:],
                 lhsT=w1_codes[:, t * P : (t + 1) * P].bitcast(FP8X4),
                 lhsT_scale=w1_scale_rows[:, t * P : (t + 1) * P],
-                rhs=x_codes[:].bitcast(FP8X4),
-                rhs_scale=x_scale_rows[:],
+                rhs=x_codes[:, j0 : j0 + n].bitcast(FP8X4),
+                rhs_scale=x_scale_rows[:, j0 : j0 + n],
                 start=True,
                 stop=True,
             )
-            y_gate[t] = tile("y_gate%d" % t, [P, S], F32)
-            nc.scalar.activation(y_gate[t][:], y[t][:], SIGMOID)
+            nc.scalar.activation(y_gate[t][:, j0 : j0 + n], y[t, j0][:], SIGMOID)
 
-        def gate_first_slots(t, slots):
-            gated1[t] = tile("gated1_%d" % t, [P, S], F32)
-            nc.vector.tensor_tensor(gated1[t][:], slots, y_gate[t][:], MULT)
+        def gate_first_slots(t, j0, n, slots=None):
+            if slots is None:
+                slots = mem_sb[t][:].indirect(entries(a1_sb, j0, n))
+            nc.vector.tensor_tensor(gated1[t][:, j0 : j0 + n], slots, y_gate[t][:, j0 : j0 + n], MULT)
 
-        def close_first_hop(t):
-            h[t] = tile("h%d" % t, [P, S], F32)
-            nc.vector.tensor_tensor(h[t][:], y[t][:], gated1[t][:], ADD)
-            bare_gate = tile("bare_gate%d" % t, [P, S], F32)
-            nc.scalar.activation(bare_gate[:], h[t][:], SIGMOID)
-            h_gate[t] = tile("h_gate%d" % t, [P, S], F32)
-            nc.scalar.activation(h_gate[t][:], bare_gate[:], COPY, scale=gn_sb[:, t : t + 1])
+        def add_first_slots(t, j0, n):
+            nc.vector.tensor_tensor(h[t][:, j0 : j0 + n], y[t, j0][:], gated1[t][:, j0 : j0 + n], ADD)
 
-        def second_hop(quarters, j0, n):
-            for t in quarters:
-                if j0 == CHUNKS[-1][0]:
-                    offset = first_grouped_at + (t - WIDE) * 4 * n
-                else:
-                    offset = gated_ring_at + (t + 2 * (j0 // HALF)) % PACK * 4 * HALF
-                gated2[t] = placed("gated2_%d_%d" % (t, j0), [P, n], F32, offset)
-                nc.vector.tensor_tensor(
-                    gated2[t][:], mem_sb[t][:].indirect(entries(a2_sb, j0, n)), h_gate[t][:, j0 : j0 + n], MULT
-                )
-            for t in quarters:
-                nc.vector.scalar_tensor_tensor(
-                    z_quarters[:, t, j0 : j0 + n], h[t][:, j0 : j0 + n], gn_sb[:, t : t + 1], gated2[t][:], MULT, ADD
-                )
+        def gate(t):
+            bare_gate[t] = tile("bare_gate%d" % t, [P, S], F32)
+            nc.scalar.activation(bare_gate[t][:], h[t][:], SIGMOID)
 
-        def group_z(j0, n, copy):
-            if j0 == 0:
-                z_grouped[j0] = placed("z_grouped%d" % j0, [P, PACK * n], BF16, first_grouped_at)
-            else:
-                z_grouped[j0] = tile("z_grouped%d" % j0, [P, PACK * n], BF16)
-            interleave(copy, z_grouped[j0][:], z_quarters[:, :, j0 : j0 + n])
-
-        def answer(j0, n, banks, copies):
-            z_codes = tile("z_codes%d" % j0, [P, n], U32)
-            z_scale_rows = tile("z_scale_rows%d" % j0, [P, n], U8)
-            nc.vector.quantize_mx(z_codes[:].bitcast(FP8X4), z_scale_rows[:], z_grouped[j0][:])
-            share = N // P // len(banks)
-            for g, (bank, copy) in enumerate(zip(banks, copies)):
-                acc = psum.tile([P, share, n], F32, name="acc%d_%d" % (j0, g), tag="bank%d" % bank)
-                for i in range(share):
-                    b = share * g + i
-                    nc.tensor.matmul_mx(
-                        acc[:, i, :],
-                        lhsT=w2_codes[:, b * P : (b + 1) * P].bitcast(FP8X4),
-                        lhsT_scale=w2_scale_rows[:, b * P : (b + 1) * P],
-                        rhs=z_codes[:].bitcast(FP8X4),
-                        rhs_scale=z_scale_rows[:],
-                        start=True,
-                        stop=True,
-                    )
-                result = tile("result%d_%d" % (j0, g), [P, share, n], F32)
-                copy(result[:], acc[:])
-                nc.sync.dma_start(
-                    out[share * g * P : share * (g + 1) * P, j0 : j0 + n].rearrange("(b p) j -> p b j", p=P),
-                    result[:],
-                )
-
-        nc.vector.tensor_copy(x_codes[:], word_table[:].bitcast(U32).indirect(offs_sb[:]))
-        nc.sync.dma_start(w2_raw[:], w2.rearrange("(p j) c -> p j c", j=PACK))
-        for t in range(PACK):
-            project(t)
-
-        first_slots = tile("first_slots", [P, S], F32)
-        nc.vector.tensor_copy(first_slots[:], mem_sb[0][:].indirect(a1_sb[:]))
-        for pair in ((0, 1), (2, 3)):
-            for t in pair:
-                gate_first_slots(t, mem_sb[t][:].indirect(a1_sb[:]) if t else first_slots[:])
-            for t in pair:
-                close_first_hop(t)
-
-        for b in range(N // P):
-            interleave(
-                nc.scalar.copy, w2_grouped[:, b * P * PACK : (b + 1) * P * PACK], w2_raw[:, :, b * P : (b + 1) * P]
+        def gain_gate(t, j0, n):
+            g, c0 = divmod(j0, HALF)
+            nc.scalar.activation(
+                h_gate[g][t][:, c0 : c0 + n], bare_gate[t][:, j0 : j0 + n], COPY, scale=gn_sb[:, t : t + 1]
             )
-        nc.vector.quantize_mx(w2_codes[:].bitcast(FP8X4), w2_scale_rows[:], w2_grouped[:])
+
+        def gain_h(g, t):
+            cols = slice(g * HALF, (g + 1) * HALF)
+            nc.scalar.activation(gained_h[g][:, t, :], h[t][:, cols], COPY, scale=gn_sb[:, t : t + 1])
+
+        def gate_second_slots(t, j0, n):
+            g, c0 = divmod(j0, HALF)
+            nc.vector.tensor_tensor(
+                gated2[g][:, t, c0 : c0 + n],
+                mem_sb[t][:].indirect(entries(a2_sb, j0, n)),
+                h_gate[g][t][:, c0 : c0 + n],
+                MULT,
+            )
+
+        def close_second_hop(j0, n):
+            g, c0 = divmod(j0, HALF)
+            z_grouped[j0] = placed("z_grouped%d" % j0, [P, PACK * n], BF16, 6 * ROW + 2 * PACK * j0)
+            nc.vector.tensor_tensor(
+                woven(z_grouped[j0][:]),
+                by_fours(gained_h[g][:, :, c0 : c0 + n]),
+                by_fours(gated2[g][:, :, c0 : c0 + n]),
+                ADD,
+            )
+
+        def group_w2(b):
+            g, c0 = divmod(b * P, N // 2)
+            nc.scalar.copy(
+                woven(w2_grouped[:, b * P * PACK : (b + 1) * P * PACK]), by_fours(w2_raw[g][:, :, c0 : c0 + P])
+            )
+
+        def quantise(j0, n):
+            z_codes[j0] = tile("z_codes%d" % j0, [P, n], U32)
+            z_scale_rows[j0] = tile("z_scale_rows%d" % j0, [P, n], U8)
+            nc.vector.quantize_mx(z_codes[j0][:].bitcast(FP8X4), z_scale_rows[j0][:], z_grouped[j0][:])
+
+        def multiply(j0, n, blocks, bank):
+            acc = psum.tile([P, len(blocks), n], F32, name="acc%d_%d" % (j0, blocks[0]), tag="bank%d" % bank)
+            for i, b in enumerate(blocks):
+                nc.tensor.matmul_mx(
+                    acc[:, i, :],
+                    lhsT=w2_codes[:, b * P : (b + 1) * P].bitcast(FP8X4),
+                    lhsT_scale=w2_scale_rows[:, b * P : (b + 1) * P],
+                    rhs=z_codes[j0][:].bitcast(FP8X4),
+                    rhs_scale=z_scale_rows[j0][:],
+                    start=True,
+                    stop=True,
+                )
+            return acc
+
+        def store(j0, n, pair, rows):
+            nc.sync.dma_start(
+                out[2 * pair * P : 2 * (pair + 1) * P, j0 : j0 + n].rearrange("(b p) j -> p b j", p=P), rows[:]
+            )
+
+        def result(name, n):
+            return tile(name, [P, 2, n], F32)
+
+        for j0 in (0, HALF):
+            nc.vector.tensor_copy(
+                x_codes[:, j0 : j0 + HALF], word_table[:].bitcast(U32).indirect(entries(offs_sb, j0, HALF))
+            )
+        nc.sync.dma_start(w2_raw[0][:], w2_rows[:, :, : N // 2])
+        nc.sync.dma_start(w2_raw[1][:], w2_rows[:, :, N // 2 :])
+        project(0, 0, HALF, 0)
+        project(0, HALF, HALF, 4)
+        for t in range(1, PACK):
+            project(t, 0, S, t)
+
+        first_slots = tile("first_slots", [P, HALF], F32)
+        nc.vector.tensor_copy(first_slots[:], mem_sb[0][:].indirect(entries(a1_sb, HALF, HALF)))
+        gate_first_slots(0, 0, HALF)
+        gate_first_slots(0, HALF, HALF, first_slots[:])
+        add_first_slots(0, 0, HALF)
+        add_first_slots(0, HALF, HALF)
+        gate_first_slots(1, 0, S)
+        for t in range(1, PACK):
+            if t + 1 < PACK:
+                gate_first_slots(t + 1, 0, S)
+            add_first_slots(t, 0, S)
+        gate(0)
+        gain_gate(0, 0, HALF)
+        gain_h(0, 0)
+        gain_gate(0, HALF, HALF)
+        gain_h(1, 0)
+        gate(1)
+        gain_gate(1, 0, HALF)
+        gain_h(0, 1)
+        group_w2(0)
+        for t in (2, 3):
+            gate(t)
+            gain_gate(t, 0, HALF)
+        group_w2(1)
+        gain_h(0, 2)
+        gain_gate(1, HALF, HALF)
+        gain_h(0, 3)
+        gain_gate(2, HALF, P)
+        group_w2(2)
+        group_w2(3)
+        gain_h(1, 1)
+        gain_h(1, 2)
+        gain_gate(3, HALF, P)
+        gain_gate(2, HALF + P, P)
+        gain_h(1, 3)
+        gain_gate(3, HALF + P, P)
 
         on_scalar, on_vector = nc.scalar.copy, nc.vector.tensor_copy
-        ways_out = (((4, 5), (on_scalar, on_scalar)), ((6,), (on_scalar,)), ((7, 0), (on_scalar, on_vector)))
-        for c, (j0, n) in enumerate(CHUNKS):
-            if j0 % HALF == 0:
-                second_hop(range(WIDE), j0, HALF)
-            second_hop(range(WIDE, PACK), j0, n)
-            group_z(j0, n, on_vector if c == len(CHUNKS) - 1 else on_scalar)
-            if c:
-                answer(*CHUNKS[c - 1], *ways_out[c - 1])
-        answer(*CHUNKS[-1], *ways_out[-1])
+        gate_second_slots(0, 0, HALF)
+        gate_second_slots(1, 0, HALF)
+        gate_second_slots(0, HALF, HALF)
+        gate_second_slots(2, 0, HALF)
+        gate_second_slots(3, 0, HALF)
+        gate_second_slots(1, HALF, HALF)
+        close_second_hop(0, HALF)
+        gate_second_slots(2, HALF, P)
+        nc.vector.quantize_mx(w2_codes[:].bitcast(FP8X4), w2_scale_rows[:], w2_grouped[:])
+        quantise(0, HALF)
+        for pair, bank in enumerate((5, 6)):
+            rows = result("a%d" % pair, HALF)
+            on_scalar(rows[:], multiply(0, HALF, (2 * pair, 2 * pair + 1), bank)[:])
+            store(0, HALF, pair, rows)
+        gate_second_slots(3, HALF, P)
+        gate_second_slots(2, HALF + P, P)
+        close_second_hop(HALF, P)
+        gate_second_slots(3, HALF + P, P)
+        quantise(HALF, P)
+        rows = result("b0", P)
+        on_scalar(rows[:], multiply(HALF, P, (0, 1), 7)[:])
+        store(HALF, P, 0, rows)
+        late = multiply(HALF, P, (2, 3), 1)
+        close_second_hop(HALF + P, P)
+        quantise(HALF + P, P)
+        rows = placed("b1", [P, 2, P], F32, 6 * ROW + 2 * PACK * (HALF + P))
+        on_vector(rows[:], late[:])
+        store(HALF, P, 1, rows)
+        for pair, banks in enumerate(((0, 4), (2, 3))):
+            rows = result("c%d" % pair, P)
+            for i, copy in enumerate((on_scalar, on_vector)):
+                copy(rows[:, i : i + 1, :], multiply(HALF + P, P, (2 * pair + i,), banks[i])[:])
+            store(HALF + P, P, pair, rows)

@@ -57,12 +57,13 @@ def tile_picked_memhop2_none_p_kernel(
         picked_scales = tile("picked_scales", [P, S], U8)
         x_scale_rows = tile("x_scale_rows", [P, S], U8)
 
-        nc.sync.dma_start(
-            scale_table[:].bitcast(I32),
-            x_scales[0].bitcast(I32).unsqueeze(1).to_broadcast([P // BLOCK, BLOCK, T // 4]),
-        )
+        w1_rows = w1.rearrange("(p j) c -> p j c", j=PACK)
+        nc.gpsimd.memset(scale_table[:, : T // 2].bitcast(I32), 0)
+        nc.vector.memset(scale_table[:, T // 2 :].bitcast(I32), 0)
+        nc.sync.dma_start(w1_raw[:, :1, :], w1_rows[:, :1, :])
         nc.sync.dma_start(offs_sb[:], offs)
-        nc.sync.dma_start(w1_raw[:], w1.rearrange("(p j) c -> p j c", j=PACK))
+        nc.sync.dma_start(scale_table[0:P:BLOCK, :].bitcast(I32), x_scales[0].bitcast(I32))
+        nc.sync.dma_start(w1_raw[:, 1:, :], w1_rows[:, 1:, :])
         nc.sync.dma_start(word_table[:], x_words[0].rearrange("p c r -> p (c r)").bitcast(I32))
         nc.sync.dma_start(a1_sb[:], a1)
         nc.sync.dma_start(a2_sb[:], a2)

@@ -104,10 +104,10 @@ def tile_picked_memhop2_none_p_kernel(
         z_grouped, z_codes, z_scale_rows = {}, {}, {}
 
         def woven(grouped):
-            return grouped.rearrange("p (c i t) -> p c t i", i=4, t=PACK)
+            return grouped.rearrange("p (c i t) -> p c t i", i=2, t=PACK)
 
-        def by_fours(quarters):
-            return quarters.rearrange("p t (c i) -> p c t i", i=4)
+        def by_pairs(quarters):
+            return quarters.rearrange("p t (c i) -> p c t i", i=2)
 
         def project(t, j0, n, bank):
             y[t, j0] = psum.tile([P, n], F32, name="y%d_%d" % (t, j0), tag="bank%d" % bank)
@@ -158,15 +158,15 @@ def tile_picked_memhop2_none_p_kernel(
             z_grouped[j0] = placed("z_grouped%d" % j0, [P, PACK * n], BF16, 6 * ROW + 2 * PACK * j0)
             nc.vector.tensor_tensor(
                 woven(z_grouped[j0][:]),
-                by_fours(gained_h[g][:, :, c0 : c0 + n]),
-                by_fours(gated2[g][:, :, c0 : c0 + n]),
+                by_pairs(gained_h[g][:, :, c0 : c0 + n]),
+                by_pairs(gated2[g][:, :, c0 : c0 + n]),
                 ADD,
             )
 
         def group_w2(b):
             g, c0 = divmod(b * P, N // 2)
             nc.scalar.copy(
-                woven(w2_grouped[:, b * P * PACK : (b + 1) * P * PACK]), by_fours(w2_raw[g][:, :, c0 : c0 + P])
+                woven(w2_grouped[:, b * P * PACK : (b + 1) * P * PACK]), by_pairs(w2_raw[g][:, :, c0 : c0 + P])
             )
 
         def quantise(j0, n):

@@ -58,8 +58,7 @@ def tile_picked_memhop2_none_p_kernel(
         x_scale_rows = tile("x_scale_rows", [P, S], U8)
 
         w1_rows = w1.rearrange("(p j) c -> p j c", j=PACK)
-        nc.gpsimd.memset(scale_table[:, : T // 2].bitcast(I32), 0)
-        nc.vector.memset(scale_table[:, T // 2 :].bitcast(I32), 0)
+        nc.vector.memset(scale_table[:].bitcast(I32), 0)
         nc.sync.dma_start(w1_raw[:, :1, :], w1_rows[:, :1, :])
         nc.sync.dma_start(offs_sb[:], offs)
         nc.sync.dma_start(scale_table[0:P:BLOCK, :].bitcast(I32), x_scales[0].bitcast(I32))

@@ -93,12 +93,13 @@ def tile_picked_memhop2_none_p_kernel(
         w2_codes = tile("w2_codes", [P, N], U32)
         w2_scale_rows = tile("w2_scale_rows", [P, N], U8)
         x_codes = tile("x_codes", [P, S], U32)
-        y, bare_gate = {}, [None] * PACK
+        y = {}
         y_gate = [tile("y_gate%d" % t, [P, S], F32) for t in range(PACK)]
         gated1 = [tile("gated1_%d" % t, [P, S], F32) for t in range(PACK)]
         h = [tile("h%d" % t, [P, S], F32) for t in range(PACK)]
-        h_gate = [[tile("h_gate%d_%d" % (g, t), [P, HALF], F32) for t in range(PACK)] for g in range(2)]
-        gained_h = [tile("gained_h%d" % g, [P, PACK, HALF], F32) for g in range(2)]
+        h_gate = [tile("h_gate%d" % t, [P, S], F32) for t in range(PACK)]
+        slots2 = [[tile("slots2_%d_%d" % (g, t), [P, HALF], F32) for t in range(PACK)] for g in range(2)]
+        gained_h = tile("gained_h", [P, PACK, S], F32)
         gated2 = [tile("gated2_%d" % g, [P, PACK, HALF], F32) for g in range(2)]
         z_grouped, z_codes, z_scale_rows = {}, {}, {}
 
@@ -126,29 +127,33 @@ def tile_picked_memhop2_none_p_kernel(
                 slots = mem_sb[t][:].indirect(entries(a1_sb, j0, n))
             nc.vector.tensor_tensor(gated1[t][:, j0 : j0 + n], slots, y_gate[t][:, j0 : j0 + n], MULT)
 
-        def add_first_slots(t, j0, n):
-            nc.vector.tensor_tensor(h[t][:, j0 : j0 + n], y[t, j0][:], gated1[t][:, j0 : j0 + n], ADD)
-
-        def gate(t):
-            bare_gate[t] = tile("bare_gate%d" % t, [P, S], F32)
-            nc.scalar.activation(bare_gate[t][:], h[t][:], SIGMOID)
-
-        def gain_gate(t, j0, n):
-            g, c0 = divmod(j0, HALF)
-            nc.scalar.activation(
-                h_gate[g][t][:, c0 : c0 + n], bare_gate[t][:, j0 : j0 + n], COPY, scale=gn_sb[:, t : t + 1]
+        def add_first_slots(t, j0, n, p0=None):
+            p0 = j0 if p0 is None else p0
+            nc.vector.tensor_tensor(
+                h[t][:, j0 : j0 + n], y[t, p0][:, j0 - p0 : j0 - p0 + n], gated1[t][:, j0 : j0 + n], ADD
             )
 
-        def gain_h(g, t):
-            cols = slice(g * HALF, (g + 1) * HALF)
-            nc.scalar.activation(gained_h[g][:, t, :], h[t][:, cols], COPY, scale=gn_sb[:, t : t + 1])
+        def gate(t, j0, n):
+            nc.scalar.activation(h_gate[t][:, j0 : j0 + n], h[t][:, j0 : j0 + n], SIGMOID)
+
+        def fetch_second_slots(g, t):
+            nc.scalar.activation(slots2[g][t][:], mem_sb[t][:].indirect(entries(a2_sb, g * HALF, HALF)), COPY)
+
+        def gain_h(t, j0, n):
+            cols = slice(j0, j0 + n)
+            nc.scalar.activation(gained_h[:, t, cols], h[t][:, cols], COPY, scale=gn_sb[:, t : t + 1])
+
+        def gain_h_aside(t):
+            nc.gpsimd.tensor_scalar(gained_h[:, t, :], h[t][:], gn_sb[:, t : t + 1], 0.0, MULT, ADD)
 
         def gate_second_slots(t, j0, n):
             g, c0 = divmod(j0, HALF)
-            nc.vector.tensor_tensor(
+            nc.vector.scalar_tensor_tensor(
                 gated2[g][:, t, c0 : c0 + n],
-                mem_sb[t][:].indirect(entries(a2_sb, j0, n)),
-                h_gate[g][t][:, c0 : c0 + n],
+                slots2[g][t][:, c0 : c0 + n],
+                gn_sb[:, t : t + 1],
+                h_gate[t][:, j0 : j0 + n],
+                MULT,
                 MULT,
             )
 
@@ -157,14 +162,14 @@ def tile_picked_memhop2_none_p_kernel(
             z_grouped[j0] = placed("z_grouped%d" % j0, [P, PACK * n], BF16, 6 * ROW + 2 * PACK * j0)
             nc.vector.tensor_tensor(
                 woven(z_grouped[j0][:]),
-                by_pairs(gained_h[g][:, :, c0 : c0 + n]),
+                by_pairs(gained_h[:, :, j0 : j0 + n]),
                 by_pairs(gated2[g][:, :, c0 : c0 + n]),
                 ADD,
             )
 
-        def group_w2(b):
+        def group_w2(b, copy):
             g, c0 = divmod(b * P, N // 2)
-            nc.scalar.copy(
+            copy(
                 woven(w2_grouped[:, b * P * PACK : (b + 1) * P * PACK]), by_pairs(w2_raw[g][:, :, c0 : c0 + P])
             )
 
@@ -211,57 +216,55 @@ def tile_picked_memhop2_none_p_kernel(
         gate_first_slots(0, 0, HALF)
         gate_first_slots(0, HALF, HALF, first_slots[:])
         add_first_slots(0, 0, HALF)
-        add_first_slots(0, HALF, HALF)
         gate_first_slots(1, 0, S)
-        for t in range(1, PACK):
-            if t + 1 < PACK:
-                gate_first_slots(t + 1, 0, S)
-            add_first_slots(t, 0, S)
-        gate(0)
-        gain_gate(0, 0, HALF)
-        gain_h(0, 0)
-        gain_gate(0, HALF, HALF)
-        gain_h(1, 0)
-        gate(1)
-        gain_gate(1, 0, HALF)
-        gain_h(0, 1)
-        group_w2(0)
-        for t in (2, 3):
-            gate(t)
-            gain_gate(t, 0, HALF)
-        group_w2(1)
-        gain_h(0, 2)
-        gain_gate(1, HALF, HALF)
-        gain_h(0, 3)
-        gain_gate(2, HALF, P)
-        group_w2(2)
-        group_w2(3)
-        gain_h(1, 1)
-        gain_h(1, 2)
-        gain_gate(3, HALF, P)
-        gain_gate(2, HALF + P, P)
-        gain_h(1, 3)
-        gain_gate(3, HALF + P, P)
+        add_first_slots(0, HALF, HALF)
+        gate_first_slots(2, 0, S)
+        add_first_slots(1, 0, S)
+        gate_first_slots(3, 0, S)
+        add_first_slots(2, 0, S)
+        add_first_slots(3, 0, S)
+        for t in range(PACK - 1):
+            gain_h_aside(t)
+
+        fetch_second_slots(0, 0)
+        fetch_second_slots(0, 1)
+        fetch_second_slots(0, 2)
+        gate(0, 0, S)
+        fetch_second_slots(0, 3)
+        gate(1, 0, S)
+        fetch_second_slots(1, 0)
+        group_w2(0, nc.scalar.copy)
+        gate(2, 0, HALF)
+        group_w2(1, nc.scalar.copy)
+        gate(3, 0, HALF)
+        gain_h(3, 0, HALF)
+        fetch_second_slots(1, 1)
+        gate(2, HALF, HALF)
+        fetch_second_slots(1, 2)
+        gate(3, HALF, HALF)
+        fetch_second_slots(1, 3)
+        gain_h(3, HALF, HALF)
 
         on_scalar, on_vector = nc.scalar.copy, nc.vector.tensor_copy
         gate_second_slots(0, 0, HALF)
         gate_second_slots(1, 0, HALF)
-        gate_second_slots(0, HALF, HALF)
         gate_second_slots(2, 0, HALF)
+        group_w2(2, on_vector)
         gate_second_slots(3, 0, HALF)
-        gate_second_slots(1, HALF, HALF)
+        group_w2(3, on_vector)
         close_second_hop(0, HALF)
-        gate_second_slots(2, HALF, P)
         nc.vector.quantize_mx(w2_codes[:].bitcast(FP8X4), w2_scale_rows[:], w2_grouped[:])
         quantise(0, HALF)
         for pair, bank in enumerate((5, 6)):
             rows = result("a%d" % pair, HALF)
             on_scalar(rows[:], multiply(0, HALF, (2 * pair, 2 * pair + 1), bank)[:])
             store(0, HALF, pair, rows)
+        gate_second_slots(0, HALF, HALF)
+        gate_second_slots(1, HALF, HALF)
+        gate_second_slots(2, HALF, HALF)
         gate_second_slots(3, HALF, P)
-        gate_second_slots(2, HALF + P, P)
-        close_second_hop(HALF, P)
         gate_second_slots(3, HALF + P, P)
+        close_second_hop(HALF, P)
         quantise(HALF, P)
         rows = result("b0", P)
         on_scalar(rows[:], multiply(HALF, P, (0, 1), 7)[:])

@@ -79,7 +79,7 @@ def tile_picked_memhop2_none_p_kernel(
         nc.sync.dma_start(mem_sb[0][:], mem_rows[:, 0, :])
         nc.sync.dma_start(mem_sb[1][:], mem_rows[:, 1, :])
 
-        w1_codes = tile("w1_codes", [P, H], U32)
+        w1_codes = placed("w1_codes", [P, H], U32, 7 * ROW)
         w1_scale_rows = tile("w1_scale_rows", [P, H], U8)
         nc.vector.tensor_copy(
             w1_grouped[:].rearrange("p (t m j) -> p m j t", t=PACK, j=PACK),
@@ -89,19 +89,29 @@ def tile_picked_memhop2_none_p_kernel(
         nc.sync.dma_start(mem_sb[3][:], mem_rows[:, 3, :])
         nc.vector.quantize_mx(w1_codes[:].bitcast(FP8X4), w1_scale_rows[:], w1_grouped[:])
 
-        w2_grouped = tile("w2_grouped", [P, PACK * N], BF16)
+        w2_grouped = placed("w2_grouped", [P, PACK * N], BF16, 9 * ROW - ROW // 4)
         w2_codes = tile("w2_codes", [P, N], U32)
         w2_scale_rows = tile("w2_scale_rows", [P, N], U8)
         x_codes = tile("x_codes", [P, S], U32)
         y = {}
         y_gate = [tile("y_gate%d" % t, [P, S], F32) for t in range(PACK)]
-        gated1 = [tile("gated1_%d" % t, [P, S], F32) for t in range(PACK)]
+        gated1 = [tile("gated1_%d" % t, [P, S], F32) for t in range(2)]
+        gated1.append(placed("gated1_2", [P, S], F32, 11 * ROW))
+        gated1.append(placed("gated1_3", [P, S], F32, 9 * ROW + ROW // 2))
         h = [tile("h%d" % t, [P, S], F32) for t in range(PACK)]
         h_gate = [tile("h_gate%d" % t, [P, S], F32) for t in range(PACK)]
-        slots2 = [[tile("slots2_%d_%d" % (g, t), [P, HALF], F32) for t in range(PACK)] for g in range(2)]
+        early_slots = placed("early_slots", [P, 3 * S], F32, 7 * ROW)
+        late_slots = placed("late_slots", [P, S], F32, 10 * ROW - ROW // 4)
         gained_h = tile("gained_h", [P, PACK, S], F32)
-        gated2 = [tile("gated2_%d" % g, [P, PACK, HALF], F32) for g in range(2)]
+        gated2 = placed("gated2", [P, PACK, S], F32, 11 * ROW)
         z_grouped, z_codes, z_scale_rows = {}, {}, {}
+
+        def slots2(t, j0, n):
+            if t < 2:
+                return early_slots[:, t * S + j0 : t * S + j0 + n]
+            if j0 < HALF:
+                return early_slots[:, 2 * S + (t - 2) * HALF + j0 : 2 * S + (t - 2) * HALF + j0 + n]
+            return late_slots[:, (t - 3) * HALF + j0 : (t - 3) * HALF + j0 + n]
 
         def woven(grouped):
             return grouped.rearrange("p (c i t) -> p c t i", i=2, t=PACK)
@@ -136,8 +146,8 @@ def tile_picked_memhop2_none_p_kernel(
         def gate(t, j0, n):
             nc.scalar.activation(h_gate[t][:, j0 : j0 + n], h[t][:, j0 : j0 + n], SIGMOID)
 
-        def fetch_second_slots(g, t):
-            nc.scalar.activation(slots2[g][t][:], mem_sb[t][:].indirect(entries(a2_sb, g * HALF, HALF)), COPY)
+        def fetch_second_slots(t, j0, n):
+            nc.scalar.activation(slots2(t, j0, n), mem_sb[t][:].indirect(entries(a2_sb, j0, n)), COPY)
 
         def gain_h(t, j0, n):
             cols = slice(j0, j0 + n)
@@ -147,31 +157,26 @@ def tile_picked_memhop2_none_p_kernel(
             nc.gpsimd.tensor_scalar(gained_h[:, t, :], h[t][:], gn_sb[:, t : t + 1], 0.0, MULT, ADD)
 
         def gate_second_slots(t, j0, n):
-            g, c0 = divmod(j0, HALF)
+            cols = slice(j0, j0 + n)
             nc.vector.scalar_tensor_tensor(
-                gated2[g][:, t, c0 : c0 + n],
-                slots2[g][t][:, c0 : c0 + n],
-                gn_sb[:, t : t + 1],
-                h_gate[t][:, j0 : j0 + n],
-                MULT,
-                MULT,
+                gated2[:, t, cols], slots2(t, j0, n), gn_sb[:, t : t + 1], h_gate[t][:, cols], MULT, MULT
             )
 
         def close_second_hop(j0, n):
-            g, c0 = divmod(j0, HALF)
             z_grouped[j0] = placed("z_grouped%d" % j0, [P, PACK * n], BF16, 6 * ROW + 2 * PACK * j0)
             nc.vector.tensor_tensor(
                 woven(z_grouped[j0][:]),
                 by_pairs(gained_h[:, :, j0 : j0 + n]),
-                by_pairs(gated2[g][:, :, c0 : c0 + n]),
+                by_pairs(gated2[:, :, j0 : j0 + n]),
                 ADD,
             )
 
-        def group_w2(b, copy):
-            g, c0 = divmod(b * P, N // 2)
-            copy(
-                woven(w2_grouped[:, b * P * PACK : (b + 1) * P * PACK]), by_pairs(w2_raw[g][:, :, c0 : c0 + P])
-            )
+        def group_w2(g, copy):
+            copy(woven(w2_grouped[:, g * 2 * N : (g + 1) * 2 * N]), by_pairs(w2_raw[g][:]))
+
+        def quantise_w2(g):
+            cols = slice(g * N // 2, (g + 1) * N // 2)
+            nc.vector.quantize_mx(w2_codes[:, cols].bitcast(FP8X4), w2_scale_rows[:, cols], w2_grouped[:, g * 2 * N : (g + 1) * 2 * N])
 
         def quantise(j0, n):
             z_codes[j0] = tile("z_codes%d" % j0, [P, n], U32)
@@ -226,55 +231,47 @@ def tile_picked_memhop2_none_p_kernel(
         for t in range(PACK - 1):
             gain_h_aside(t)
 
-        fetch_second_slots(0, 0)
-        fetch_second_slots(0, 1)
-        fetch_second_slots(0, 2)
+        on_scalar, on_vector = nc.scalar.copy, nc.vector.tensor_copy
+        fetch_second_slots(0, 0, S)
         gate(0, 0, S)
-        fetch_second_slots(0, 3)
+        fetch_second_slots(1, 0, S)
+        fetch_second_slots(2, 0, HALF)
+        fetch_second_slots(3, 0, HALF)
         gate(1, 0, S)
-        fetch_second_slots(1, 0)
-        group_w2(0, nc.scalar.copy)
-        gate(2, 0, HALF)
-        group_w2(1, nc.scalar.copy)
+        gate(2, 0, S)
         gate(3, 0, HALF)
         gain_h(3, 0, HALF)
-        fetch_second_slots(1, 1)
-        gate(2, HALF, HALF)
-        fetch_second_slots(1, 2)
+        fetch_second_slots(3, HALF, HALF)
         gate(3, HALF, HALF)
-        fetch_second_slots(1, 3)
+        fetch_second_slots(2, HALF, HALF)
+        group_w2(1, on_scalar)
         gain_h(3, HALF, HALF)
 
-        on_scalar, on_vector = nc.scalar.copy, nc.vector.tensor_copy
-        gate_second_slots(0, 0, HALF)
-        gate_second_slots(1, 0, HALF)
+        gate_second_slots(0, 0, S)
+        gate_second_slots(1, 0, S)
         gate_second_slots(2, 0, HALF)
-        group_w2(2, on_vector)
         gate_second_slots(3, 0, HALF)
-        group_w2(3, on_vector)
+        group_w2(0, on_vector)
         close_second_hop(0, HALF)
-        nc.vector.quantize_mx(w2_codes[:].bitcast(FP8X4), w2_scale_rows[:], w2_grouped[:])
+        quantise_w2(0)
         quantise(0, HALF)
+        gate_second_slots(3, HALF, P)
+        gate_second_slots(2, HALF, P)
+        quantise_w2(1)
+        close_second_hop(HALF, P)
+        gate_second_slots(3, HALF + P, P)
+        gate_second_slots(2, HALF + P, P)
+        quantise(HALF, P)
+        close_second_hop(HALF + P, P)
+        quantise(HALF + P, P)
         for pair, bank in enumerate((5, 6)):
             rows = result("a%d" % pair, HALF)
             on_scalar(rows[:], multiply(0, HALF, (2 * pair, 2 * pair + 1), bank)[:])
             store(0, HALF, pair, rows)
-        gate_second_slots(0, HALF, HALF)
-        gate_second_slots(1, HALF, HALF)
-        gate_second_slots(2, HALF, HALF)
-        gate_second_slots(3, HALF, P)
-        gate_second_slots(3, HALF + P, P)
-        close_second_hop(HALF, P)
-        quantise(HALF, P)
-        rows = result("b0", P)
-        on_scalar(rows[:], multiply(HALF, P, (0, 1), 7)[:])
-        store(HALF, P, 0, rows)
-        late = multiply(HALF, P, (2, 3), 1)
-        close_second_hop(HALF + P, P)
-        quantise(HALF + P, P)
-        rows = placed("b1", [P, 2, P], F32, 6 * ROW + 2 * PACK * (HALF + P))
-        on_vector(rows[:], late[:])
-        store(HALF, P, 1, rows)
+        for pair, bank in enumerate((7, 1)):
+            rows = result("b%d" % pair, P)
+            on_scalar(rows[:], multiply(HALF, P, (2 * pair, 2 * pair + 1), bank)[:])
+            store(HALF, P, pair, rows)
         for pair, banks in enumerate(((0, 4), (2, 3))):
             rows = result("c%d" % pair, P)
             for i, copy in enumerate((on_scalar, on_vector)):

@@ -49,9 +49,11 @@ def tile_picked_memhop2_none_p_kernel(
         a2_sb = tile("a2_sb", [P, S // GROUP], U16)
         scale_table = placed("scale_table", [P, T], U8, ROW - T // 2)
         w1_raw = placed("w1_raw", [P, PACK, H], F32, 2 * ROW)
-        word_table = placed("word_table", [P, T], I32, 4 * ROW)
-        mem_sb = [placed("mem%d" % t, [P, U], F32, row * ROW) for t, row in enumerate((0, 1, 2, 3))]
-        w2_raw = [placed("w2_raw%d" % g, [P, PACK, N // 2], F32, row * ROW) for g, row in enumerate((4, 5))]
+        word_table = placed("word_table", [P, T], I32, 13 * ROW)
+        mem_at = (0, 2 * ROW, 3 * ROW, 13 * ROW)
+        mem_sb = [placed("mem%d" % t, [P, U], F32, at) for t, at in enumerate(mem_at)]
+        w2_first_raw = placed("w2_first_raw", [P, PACK, P], F32, ROW)
+        w2_raw = placed("w2_raw", [P, PACK, N - P], F32, 14 * ROW)
         w1_grouped = tile("w1_grouped", [P, PACK * H], BF16)
         gn_sb = tile("gn_sb", [P, PACK], F32)
         picked_scales = tile("picked_scales", [P, S], U8)
@@ -61,12 +63,12 @@ def tile_picked_memhop2_none_p_kernel(
         nc.vector.memset(scale_table[:].bitcast(I32), 0)
         nc.sync.dma_start(w1_raw[:, :1, :], w1_rows[:, :1, :])
         nc.sync.dma_start(offs_sb[:], offs)
-        nc.sync.dma_start(scale_table[0:P:BLOCK, :].bitcast(I32), x_scales[0].bitcast(I32))
-        nc.sync.dma_start(w1_raw[:, 1:, :], w1_rows[:, 1:, :])
-        nc.sync.dma_start(word_table[:], x_words[0].rearrange("p c r -> p (c r)").bitcast(I32))
         nc.sync.dma_start(a1_sb[:], a1)
         nc.sync.dma_start(a2_sb[:], a2)
         nc.sync.dma_start(gn_sb[:], gn.rearrange("(p t) o -> p (t o)", t=PACK))
+        nc.sync.dma_start(scale_table[0:P:BLOCK, :].bitcast(I32), x_scales[0].bitcast(I32))
+        nc.sync.dma_start(w1_raw[:, 1:, :], w1_rows[:, 1:, :])
+        nc.sync.dma_start(word_table[:], x_words[0].rearrange("p c r -> p (c r)").bitcast(I32))
 
         nc.vector.tensor_copy(picked_scales[:], scale_table[:].indirect(offs_sb[:]))
         nc.vector.tensor_copy(x_scale_rows[:].bitcast(I32), picked_scales[:].bitcast(I32))
@@ -77,7 +79,7 @@ def tile_picked_memhop2_none_p_kernel(
         mem_rows = mem.rearrange("(p t) u -> p t u", t=PACK)
         w2_rows = w2.rearrange("(p j) c -> p j c", j=PACK)
         nc.sync.dma_start(mem_sb[0][:], mem_rows[:, 0, :])
-        nc.sync.dma_start(mem_sb[1][:], mem_rows[:, 1, :])
+        nc.sync.dma_start(w2_first_raw[:], w2_rows[:, :, :P])
 
         w1_codes = placed("w1_codes", [P, H], U32, 7 * ROW)
         w1_scale_rows = tile("w1_scale_rows", [P, H], U8)
@@ -85,23 +87,25 @@ def tile_picked_memhop2_none_p_kernel(
             w1_grouped[:].rearrange("p (t m j) -> p m j t", t=PACK, j=PACK),
             w1_raw[:].rearrange("p j (m t) -> p m j t", t=PACK),
         )
+        nc.sync.dma_start(mem_sb[1][:], mem_rows[:, 1, :])
         nc.sync.dma_start(mem_sb[2][:], mem_rows[:, 2, :])
-        nc.sync.dma_start(mem_sb[3][:], mem_rows[:, 3, :])
         nc.vector.quantize_mx(w1_codes[:].bitcast(FP8X4), w1_scale_rows[:], w1_grouped[:])
 
-        w2_grouped = placed("w2_grouped", [P, PACK * N], BF16, 9 * ROW - ROW // 4)
+        w2_first_grouped = placed("w2_first_grouped", [P, PACK * P], BF16, 4 * ROW)
+        w2_grouped = placed("w2_grouped", [P, PACK * (N - P)], BF16, 9 * ROW - ROW // 8)
         w2_codes = tile("w2_codes", [P, N], U32)
-        w2_scale_rows = tile("w2_scale_rows", [P, N], U8)
+        w2_scale_rows = placed("w2_scale_rows", [P, N], U8, 9 * ROW + 5 * ROW // 8)
         x_codes = tile("x_codes", [P, S], U32)
         y = {}
         y_gate = [tile("y_gate%d" % t, [P, S], F32) for t in range(PACK)]
+        first_gate = placed("first_gate", [P, HALF], F32, 4 * ROW)
         gated1 = [tile("gated1_%d" % t, [P, S], F32) for t in range(2)]
         gated1.append(placed("gated1_2", [P, S], F32, 11 * ROW))
         gated1.append(placed("gated1_3", [P, S], F32, 9 * ROW + ROW // 2))
         h = [tile("h%d" % t, [P, S], F32) for t in range(PACK)]
         h_gate = [tile("h_gate%d" % t, [P, S], F32) for t in range(PACK)]
         early_slots = placed("early_slots", [P, 3 * S], F32, 7 * ROW)
-        late_slots = placed("late_slots", [P, S], F32, 10 * ROW - ROW // 4)
+        late_slots = placed("late_slots", [P, S], F32, 10 * ROW - ROW // 8)
         gained_h = tile("gained_h", [P, PACK, S], F32)
         gated2 = placed("gated2", [P, PACK, S], F32, 11 * ROW)
         z_grouped, z_codes, z_scale_rows = {}, {}, {}
@@ -112,6 +116,9 @@ def tile_picked_memhop2_none_p_kernel(
             if j0 < HALF:
                 return early_slots[:, 2 * S + (t - 2) * HALF + j0 : 2 * S + (t - 2) * HALF + j0 + n]
             return late_slots[:, (t - 3) * HALF + j0 : (t - 3) * HALF + j0 + n]
+
+        def y_gate_cols(t, j0, n):
+            return first_gate[:] if (t, j0) == (0, 0) else y_gate[t][:, j0 : j0 + n]
 
         def woven(grouped):
             return grouped.rearrange("p (c i t) -> p c t i", i=2, t=PACK)
@@ -130,12 +137,12 @@ def tile_picked_memhop2_none_p_kernel(
                 start=True,
                 stop=True,
             )
-            nc.scalar.activation(y_gate[t][:, j0 : j0 + n], y[t, j0][:], SIGMOID)
+            nc.scalar.activation(y_gate_cols(t, j0, n), y[t, j0][:], SIGMOID)
 
         def gate_first_slots(t, j0, n, slots=None):
             if slots is None:
                 slots = mem_sb[t][:].indirect(entries(a1_sb, j0, n))
-            nc.vector.tensor_tensor(gated1[t][:, j0 : j0 + n], slots, y_gate[t][:, j0 : j0 + n], MULT)
+            nc.vector.tensor_tensor(gated1[t][:, j0 : j0 + n], slots, y_gate_cols(t, j0, n), MULT)
 
         def add_first_slots(t, j0, n, p0=None):
             p0 = j0 if p0 is None else p0
@@ -171,12 +178,24 @@ def tile_picked_memhop2_none_p_kernel(
                 ADD,
             )
 
-        def group_w2(g, copy):
-            copy(woven(w2_grouped[:, g * 2 * N : (g + 1) * 2 * N]), by_pairs(w2_raw[g][:]))
+        def group_w2(b, blocks, copy):
+            c0, n = (b - 1) * P, blocks * P
+            copy(woven(w2_grouped[:, c0 * PACK : (c0 + n) * PACK]), by_pairs(w2_raw[:, :, c0 : c0 + n]))
 
-        def quantise_w2(g):
-            cols = slice(g * N // 2, (g + 1) * N // 2)
-            nc.vector.quantize_mx(w2_codes[:, cols].bitcast(FP8X4), w2_scale_rows[:, cols], w2_grouped[:, g * 2 * N : (g + 1) * 2 * N])
+        def group_first_w2():
+            nc.gpsimd.tensor_scalar(
+                w2_first_grouped[:].rearrange("p (c t) -> p c t", t=PACK),
+                w2_first_raw[:].rearrange("p t c -> p c t"),
+                1.0,
+                0.0,
+                MULT,
+                ADD,
+            )
+
+        def quantise_w2(b, blocks):
+            cols = slice(b * P, (b + blocks) * P)
+            grouped = w2_grouped[:, (b - 1) * P * PACK : (b - 1 + blocks) * P * PACK] if b else w2_first_grouped[:]
+            nc.vector.quantize_mx(w2_codes[:, cols].bitcast(FP8X4), w2_scale_rows[:, cols], grouped)
 
         def quantise(j0, n):
             z_codes[j0] = tile("z_codes%d" % j0, [P, n], U32)
@@ -209,8 +228,8 @@ def tile_picked_memhop2_none_p_kernel(
             nc.vector.tensor_copy(
                 x_codes[:, j0 : j0 + HALF], word_table[:].bitcast(U32).indirect(entries(offs_sb, j0, HALF))
             )
-        nc.sync.dma_start(w2_raw[0][:], w2_rows[:, :, : N // 2])
-        nc.sync.dma_start(w2_raw[1][:], w2_rows[:, :, N // 2 :])
+        nc.sync.dma_start(mem_sb[3][:], mem_rows[:, 3, :])
+        nc.sync.dma_start(w2_raw[:], w2_rows[:, :, P:])
         project(0, 0, HALF, 0)
         project(0, HALF, HALF, 4)
         for t in range(1, PACK):
@@ -221,13 +240,13 @@ def tile_picked_memhop2_none_p_kernel(
         gate_first_slots(0, 0, HALF)
         gate_first_slots(0, HALF, HALF, first_slots[:])
         add_first_slots(0, 0, HALF)
-        gate_first_slots(1, 0, S)
         add_first_slots(0, HALF, HALF)
-        gate_first_slots(2, 0, S)
-        add_first_slots(1, 0, S)
-        gate_first_slots(3, 0, S)
-        add_first_slots(2, 0, S)
-        add_first_slots(3, 0, S)
+        for t in range(1, PACK):
+            for j0 in (0, HALF):
+                gate_first_slots(t, j0, HALF)
+            for j0 in (0, HALF):
+                add_first_slots(t, j0, HALF, 0)
+        group_first_w2()
         for t in range(PACK - 1):
             gain_h_aside(t)
 
@@ -244,20 +263,21 @@ def tile_picked_memhop2_none_p_kernel(
         fetch_second_slots(3, HALF, HALF)
         gate(3, HALF, HALF)
         fetch_second_slots(2, HALF, HALF)
-        group_w2(1, on_scalar)
+        group_w2(2, 2, on_scalar)
         gain_h(3, HALF, HALF)
 
         gate_second_slots(0, 0, S)
         gate_second_slots(1, 0, S)
         gate_second_slots(2, 0, HALF)
         gate_second_slots(3, 0, HALF)
-        group_w2(0, on_vector)
+        group_w2(1, 1, on_vector)
         close_second_hop(0, HALF)
-        quantise_w2(0)
+        quantise_w2(0, 1)
+        quantise_w2(1, 1)
         quantise(0, HALF)
         gate_second_slots(3, HALF, P)
         gate_second_slots(2, HALF, P)
-        quantise_w2(1)
+        quantise_w2(2, 2)
         close_second_hop(HALF, P)
         gate_second_slots(3, HALF + P, P)
         gate_second_slots(2, HALF + P, P)

@@ -107,7 +107,7 @@ def tile_picked_memhop2_none_p_kernel(
         early_slots = placed("early_slots", [P, 3 * S], F32, 7 * ROW)
         late_slots = placed("late_slots", [P, S], F32, 10 * ROW - ROW // 8)
         gained_h = tile("gained_h", [P, PACK, S], F32)
-        gated2 = placed("gated2", [P, PACK, S], F32, 11 * ROW)
+        gated2 = placed("gated2", [P, PACK * S], F32, 11 * ROW)
         z_grouped, z_codes, z_scale_rows = {}, {}, {}
 
         def slots2(t, j0, n):
@@ -163,18 +163,25 @@ def tile_picked_memhop2_none_p_kernel(
         def gain_h_aside(t):
             nc.gpsimd.tensor_scalar(gained_h[:, t, :], h[t][:], gn_sb[:, t : t + 1], 0.0, MULT, ADD)
 
+        def chunk_of_gated2(j0, n):
+            return gated2[:, PACK * j0 : PACK * (j0 + n)].rearrange("p (t c) -> p t c", t=PACK)
+
         def gate_second_slots(t, j0, n):
-            cols = slice(j0, j0 + n)
-            nc.vector.scalar_tensor_tensor(
-                gated2[:, t, cols], slots2(t, j0, n), gn_sb[:, t : t + 1], h_gate[t][:, cols], MULT, MULT
-            )
+            slots, gates = slots2(t, j0, n), h_gate[t][:, j0 : j0 + n]
+            if j0 == HALF and n == HALF:
+                both = gated2[:, PACK * HALF :].rearrange("p (g t c) -> p t g c", g=2, t=PACK)
+                gated = both[:, t, :, :]
+                slots, gates = (x.rearrange("p (g c) -> p g c", g=2) for x in (slots, gates))
+            else:
+                gated = chunk_of_gated2(j0, n)[:, t, :]
+            nc.vector.scalar_tensor_tensor(gated, slots, gn_sb[:, t : t + 1], gates, MULT, MULT)
 
         def close_second_hop(j0, n):
             z_grouped[j0] = placed("z_grouped%d" % j0, [P, PACK * n], BF16, 6 * ROW + 2 * PACK * j0)
             nc.vector.tensor_tensor(
                 woven(z_grouped[j0][:]),
                 by_pairs(gained_h[:, :, j0 : j0 + n]),
-                by_pairs(gated2[:, :, j0 : j0 + n]),
+                by_pairs(chunk_of_gated2(j0, n)),
                 ADD,
             )
 
@@ -262,28 +269,30 @@ def tile_picked_memhop2_none_p_kernel(
         gain_h(3, 0, HALF)
         fetch_second_slots(3, HALF, HALF)
         gate(3, HALF, HALF)
-        fetch_second_slots(2, HALF, HALF)
         group_w2(2, 2, on_scalar)
+        fetch_second_slots(2, HALF, HALF)
         gain_h(3, HALF, HALF)
 
-        gate_second_slots(0, 0, S)
-        gate_second_slots(1, 0, S)
-        gate_second_slots(2, 0, HALF)
-        gate_second_slots(3, 0, HALF)
+        middle, last = HALF, HALF + P
+        for t in range(PACK):
+            gate_second_slots(t, 0, HALF)
         group_w2(1, 1, on_vector)
         close_second_hop(0, HALF)
         quantise_w2(0, 1)
         quantise_w2(1, 1)
         quantise(0, HALF)
-        gate_second_slots(3, HALF, P)
-        gate_second_slots(2, HALF, P)
+        for t in (0, 1, 3):
+            gate_second_slots(t, middle, P)
         quantise_w2(2, 2)
-        close_second_hop(HALF, P)
-        gate_second_slots(3, HALF + P, P)
-        gate_second_slots(2, HALF + P, P)
-        quantise(HALF, P)
-        close_second_hop(HALF + P, P)
-        quantise(HALF + P, P)
+        gate_second_slots(2, middle, P)
+        gate_second_slots(0, last, P)
+        gate_second_slots(1, last, P)
+        close_second_hop(middle, P)
+        gate_second_slots(2, last, P)
+        gate_second_slots(3, last, P)
+        quantise(middle, P)
+        close_second_hop(last, P)
+        quantise(last, P)
         for pair, bank in enumerate((5, 6)):
             rows = result("a%d" % pair, HALF)
             on_scalar(rows[:], multiply(0, HALF, (2 * pair, 2 * pair + 1), bank)[:])

@@ -105,12 +105,15 @@ def tile_picked_memhop2_none_p_kernel(
         h = [tile("h%d" % t, [P, S], F32) for t in range(PACK)]
         h_gate = [tile("h_gate%d" % t, [P, S], F32) for t in range(PACK)]
         early_slots = placed("early_slots", [P, 3 * S], F32, 7 * ROW)
+        earliest_slots = tile("earliest_slots", [P, HALF], F32)
         late_slots = placed("late_slots", [P, S], F32, 10 * ROW - ROW // 8)
         gained_h = tile("gained_h", [P, PACK, S], F32)
         gated2 = placed("gated2", [P, PACK * S], F32, 11 * ROW)
         z_grouped, z_codes, z_scale_rows = {}, {}, {}
 
         def slots2(t, j0, n):
+            if t == 0 and j0 < HALF:
+                return earliest_slots[:, j0 : j0 + n]
             if t < 2:
                 return early_slots[:, t * S + j0 : t * S + j0 + n]
             if j0 < HALF:
@@ -126,7 +129,7 @@ def tile_picked_memhop2_none_p_kernel(
         def by_pairs(quarters):
             return quarters.rearrange("p t (c i) -> p c t i", i=2)
 
-        def project(t, j0, n, bank):
+        def project(t, j0, n, bank, pieces=1):
             y[t, j0] = psum.tile([P, n], F32, name="y%d_%d" % (t, j0), tag="bank%d" % bank)
             nc.tensor.matmul_mx(
                 y[t, j0][:],
@@ -137,7 +140,9 @@ def tile_picked_memhop2_none_p_kernel(
                 start=True,
                 stop=True,
             )
-            nc.scalar.activation(y_gate_cols(t, j0, n), y[t, j0][:], SIGMOID)
+            width = n // pieces
+            for c0 in range(0, n, width):
+                nc.scalar.activation(y_gate_cols(t, j0 + c0, width), y[t, j0][:, c0 : c0 + width], SIGMOID)
 
         def gate_first_slots(t, j0, n, slots=None):
             if slots is None:
@@ -239,7 +244,9 @@ def tile_picked_memhop2_none_p_kernel(
         nc.sync.dma_start(w2_raw[:], w2_rows[:, :, P:])
         project(0, 0, HALF, 0)
         project(0, HALF, HALF, 4)
-        for t in range(1, PACK):
+        fetch_second_slots(0, 0, HALF)
+        project(1, 0, S, 1, 2)
+        for t in (2, 3):
             project(t, 0, S, t)
 
         first_slots = tile("first_slots", [P, HALF], F32)
@@ -258,7 +265,7 @@ def tile_picked_memhop2_none_p_kernel(
             gain_h_aside(t)
 
         on_scalar, on_vector = nc.scalar.copy, nc.vector.tensor_copy
-        fetch_second_slots(0, 0, S)
+        fetch_second_slots(0, HALF, HALF)
         gate(0, 0, S)
         fetch_second_slots(1, 0, S)
         fetch_second_slots(2, 0, HALF)

@@ -52,23 +52,23 @@ def tile_picked_memhop2_none_p_kernel(
         word_table = placed("word_table", [P, T], I32, 13 * ROW)
         mem_at = (0, 2 * ROW, 3 * ROW, 13 * ROW)
         mem_sb = [placed("mem%d" % t, [P, U], F32, at) for t, at in enumerate(mem_at)]
-        w2_first_raw = placed("w2_first_raw", [P, PACK, P], F32, ROW)
+        w2_first_raw = placed("w2_first_raw", [P, PACK, P], F32, ROW + 64)
         w2_raw = placed("w2_raw", [P, PACK, N - P], F32, 14 * ROW)
         w1_grouped = tile("w1_grouped", [P, PACK * H], BF16)
-        gn_sb = tile("gn_sb", [P, PACK], F32)
+        gn_sb = placed("gn_sb", [P, PACK], F32, ROW)
         picked_scales = tile("picked_scales", [P, S], U8)
         x_scale_rows = tile("x_scale_rows", [P, S], U8)
 
         w1_rows = w1.rearrange("(p j) c -> p j c", j=PACK)
         nc.vector.memset(scale_table[:].bitcast(I32), 0)
         nc.sync.dma_start(w1_raw[:, :1, :], w1_rows[:, :1, :])
+        words = x_words[0].rearrange("p c r -> p (c r)").bitcast(I32)
         nc.sync.dma_start(offs_sb[:], offs)
-        nc.sync.dma_start(a1_sb[:], a1)
-        nc.sync.dma_start(a2_sb[:], a2)
-        nc.sync.dma_start(gn_sb[:], gn.rearrange("(p t) o -> p (t o)", t=PACK))
         nc.sync.dma_start(scale_table[0:P:BLOCK, :].bitcast(I32), x_scales[0].bitcast(I32))
         nc.sync.dma_start(w1_raw[:, 1:, :], w1_rows[:, 1:, :])
-        nc.sync.dma_start(word_table[:], x_words[0].rearrange("p c r -> p (c r)").bitcast(I32))
+        nc.sync.dma_start(word_table[:], words)
+        nc.sync.dma_start(a1_sb[:], a1)
+        nc.sync.dma_start(a2_sb[:], a2)
 
         nc.vector.tensor_copy(picked_scales[:], scale_table[:].indirect(offs_sb[:]))
         nc.vector.tensor_copy(x_scale_rows[:].bitcast(I32), picked_scales[:].bitcast(I32))
@@ -80,6 +80,7 @@ def tile_picked_memhop2_none_p_kernel(
         w2_rows = w2.rearrange("(p j) c -> p j c", j=PACK)
         nc.sync.dma_start(mem_sb[0][:], mem_rows[:, 0, :])
         nc.sync.dma_start(w2_first_raw[:], w2_rows[:, :, :P])
+        nc.sync.dma_start(gn_sb[:], gn.rearrange("(p t) o -> p (t o)", t=PACK))
 
         w1_codes = placed("w1_codes", [P, H], U32, 7 * ROW)
         w1_scale_rows = tile("w1_scale_rows", [P, H], U8)
@@ -102,13 +103,14 @@ def tile_picked_memhop2_none_p_kernel(
         gated1 = [tile("gated1_%d" % t, [P, S], F32) for t in range(2)]
         gated1.append(placed("gated1_2", [P, S], F32, 11 * ROW))
         gated1.append(placed("gated1_3", [P, S], F32, 9 * ROW + ROW // 2))
-        h = [tile("h%d" % t, [P, S], F32) for t in range(PACK)]
+        h = {t: tile("h%d" % t, [P, S], F32) for t in (0, 1, 3)}
+        h[2] = placed("h2", [P, S], F32, 12 * ROW)
         h_gate = [tile("h_gate%d" % t, [P, S], F32) for t in range(PACK)]
         early_slots = placed("early_slots", [P, 3 * S], F32, 7 * ROW)
         earliest_slots = tile("earliest_slots", [P, HALF], F32)
         late_slots = placed("late_slots", [P, S], F32, 10 * ROW - ROW // 8)
         gained_h = tile("gained_h", [P, PACK, S], F32)
-        gated2 = placed("gated2", [P, PACK * S], F32, 11 * ROW)
+        gated2 = [placed("gated2_%d" % g, [P, PACK * HALF], F32, (11 + g) * ROW) for g in range(2)]
         z_grouped, z_codes, z_scale_rows = {}, {}, {}
 
         def slots2(t, j0, n):
@@ -169,12 +171,13 @@ def tile_picked_memhop2_none_p_kernel(
             nc.gpsimd.tensor_scalar(gained_h[:, t, :], h[t][:], gn_sb[:, t : t + 1], 0.0, MULT, ADD)
 
         def chunk_of_gated2(j0, n):
-            return gated2[:, PACK * j0 : PACK * (j0 + n)].rearrange("p (t c) -> p t c", t=PACK)
+            c0 = j0 % HALF
+            return gated2[j0 // HALF][:, PACK * c0 : PACK * (c0 + n)].rearrange("p (t c) -> p t c", t=PACK)
 
         def gate_second_slots(t, j0, n):
             slots, gates = slots2(t, j0, n), h_gate[t][:, j0 : j0 + n]
             if j0 == HALF and n == HALF:
-                both = gated2[:, PACK * HALF :].rearrange("p (g t c) -> p t g c", g=2, t=PACK)
+                both = gated2[1][:].rearrange("p (g t c) -> p t g c", g=2, t=PACK)
                 gated = both[:, t, :, :]
                 slots, gates = (x.rearrange("p (g c) -> p g c", g=2) for x in (slots, gates))
             else:

@@ -123,7 +123,7 @@ def tile_picked_memhop2_none_p_kernel(
             return late_slots[:, (t - 3) * HALF + j0 : (t - 3) * HALF + j0 + n]
 
         def y_gate_cols(t, j0, n):
-            return first_gate[:] if (t, j0) == (0, 0) else y_gate[t][:, j0 : j0 + n]
+            return (first_gate if t == 0 and j0 < HALF else y_gate[t])[:, j0 : j0 + n]
 
         def woven(grouped):
             return grouped.rearrange("p (c i t) -> p c t i", i=2, t=PACK)
@@ -245,7 +245,8 @@ def tile_picked_memhop2_none_p_kernel(
             )
         nc.sync.dma_start(mem_sb[3][:], mem_rows[:, 3, :])
         nc.sync.dma_start(w2_raw[:], w2_rows[:, :, P:])
-        project(0, 0, HALF, 0)
+        project(0, 0, P, 0)
+        project(0, P, P, 5)
         project(0, HALF, HALF, 4)
         fetch_second_slots(0, 0, HALF)
         project(1, 0, S, 1, 2)
@@ -254,9 +255,11 @@ def tile_picked_memhop2_none_p_kernel(
 
         first_slots = tile("first_slots", [P, HALF], F32)
         nc.vector.tensor_copy(first_slots[:], mem_sb[0][:].indirect(entries(a1_sb, HALF, HALF)))
-        gate_first_slots(0, 0, HALF)
+        gate_first_slots(0, 0, P)
+        gate_first_slots(0, P, P)
         gate_first_slots(0, HALF, HALF, first_slots[:])
-        add_first_slots(0, 0, HALF)
+        add_first_slots(0, 0, P)
+        add_first_slots(0, P, P)
         add_first_slots(0, HALF, HALF)
         for t in range(1, PACK):
             for j0 in (0, HALF):

@@ -199,8 +199,8 @@ def tile_picked_memhop2_none_p_kernel(
 
         def group_first_w2():
             nc.gpsimd.tensor_scalar(
-                w2_first_grouped[:].rearrange("p (c t) -> p c t", t=PACK),
-                w2_first_raw[:].rearrange("p t c -> p c t"),
+                woven(w2_first_grouped[:]),
+                by_pairs(w2_first_raw[:]),
                 1.0,
                 0.0,
                 MULT,

@@ -245,9 +245,8 @@ def tile_picked_memhop2_none_p_kernel(
             )
         nc.sync.dma_start(mem_sb[3][:], mem_rows[:, 3, :])
         nc.sync.dma_start(w2_raw[:], w2_rows[:, :, P:])
-        project(0, 0, P, 0)
-        project(0, P, P, 5)
-        project(0, HALF, HALF, 4)
+        for piece, bank in enumerate((0, 5, 4, 6)):
+            project(0, piece * P, P, bank)
         fetch_second_slots(0, 0, HALF)
         project(1, 0, S, 1, 2)
         for t in (2, 3):
@@ -257,10 +256,10 @@ def tile_picked_memhop2_none_p_kernel(
         nc.vector.tensor_copy(first_slots[:], mem_sb[0][:].indirect(entries(a1_sb, HALF, HALF)))
         gate_first_slots(0, 0, P)
         gate_first_slots(0, P, P)
-        gate_first_slots(0, HALF, HALF, first_slots[:])
-        add_first_slots(0, 0, P)
-        add_first_slots(0, P, P)
-        add_first_slots(0, HALF, HALF)
+        gate_first_slots(0, HALF, P, first_slots[:, :P])
+        gate_first_slots(0, HALF + P, P, first_slots[:, P:])
+        for j0 in range(0, S, P):
+            add_first_slots(0, j0, P)
         for t in range(1, PACK):
             for j0 in (0, HALF):
                 gate_first_slots(t, j0, HALF)

from contextlib import ExitStack

import concourse.mybir as mybir

F32 = mybir.dt.float32
BF16 = mybir.dt.bfloat16
I32 = mybir.dt.int32
U32 = mybir.dt.uint32
U16 = mybir.dt.uint16
U8 = mybir.dt.uint8
FP8X4 = mybir.dt.float8_e4m3fn_x4
MULT = mybir.AluOpType.mult
ADD = mybir.AluOpType.add
SIGMOID = mybir.ActivationFunctionType.Sigmoid
COPY = mybir.ActivationFunctionType.Copy

P = 128
PACK = 4
GROUP = 16
QUADRANT = 32
BLOCK = 8
K, T, S, H, N, U = 512, 2048, 512, 512, 512, 1024
FLOPS = 2 * K * H * S + 2 * H * N * S

HALF = S // 2
ROW = 4 * U


def tile_picked_memhop2_none_p_kernel(
    tc, x_words, x_scales, w1, mem, gn, w2, offs, a1, a2, out
):
    nc = tc.nc
    with ExitStack() as ctx:
        keep = ctx.enter_context(tc.tile_pool(name="keep", bufs=1))
        psum = ctx.enter_context(tc.psum_pool(name="psum", bufs=1))
        reuse = ctx.enter_context(tc.tile_pool(name="reuse", bufs=1))

        def tile(name, shape, dtype):
            return keep.tile(shape, dtype, name=name, align_bytes=64)

        def placed(name, shape, dtype, offset):
            return reuse.tile(shape, dtype, name=name, align_bytes=64, offset=offset)

        def entries(lists, j0, n):
            return lists[:, j0 // GROUP : (j0 + n) // GROUP]

        offs_sb = tile("offs_sb", [P, S // GROUP], U16)
        a1_sb = tile("a1_sb", [P, S // GROUP], U16)
        a2_sb = tile("a2_sb", [P, S // GROUP], U16)
        scale_table = placed("scale_table", [P, T], U8, ROW - T // 2)
        w1_raw = placed("w1_raw", [P, PACK, H], F32, 2 * ROW)
        word_table = placed("word_table", [P, T], I32, 13 * ROW)
        mem_at = (0, 2 * ROW, 3 * ROW, 13 * ROW)
        mem_sb = [placed("mem%d" % t, [P, U], F32, at) for t, at in enumerate(mem_at)]
        w2_first_raw = placed("w2_first_raw", [P, PACK, P], F32, ROW + 64)
        w2_raw = placed("w2_raw", [P, PACK, N - P], F32, 14 * ROW)
        w1_grouped = tile("w1_grouped", [P, PACK * H], BF16)
        gn_sb = placed("gn_sb", [P, PACK], F32, ROW)
        picked_scales = tile("picked_scales", [P, S], U8)
        x_scale_rows = tile("x_scale_rows", [P, S], U8)

        w1_rows = w1.rearrange("(p j) c -> p j c", j=PACK)
        nc.vector.memset(scale_table[:].bitcast(I32), 0)
        nc.sync.dma_start(w1_raw[:, :1, :], w1_rows[:, :1, :])
        words = x_words[0].rearrange("p c r -> p (c r)").bitcast(I32)
        nc.sync.dma_start(offs_sb[:], offs)
        nc.sync.dma_start(scale_table[0:P:BLOCK, :].bitcast(I32), x_scales[0].bitcast(I32))
        nc.sync.dma_start(w1_raw[:, 1:, :], w1_rows[:, 1:, :])
        nc.sync.dma_start(word_table[:], words)
        nc.sync.dma_start(a1_sb[:], a1)
        nc.sync.dma_start(a2_sb[:], a2)

        nc.vector.tensor_copy(picked_scales[:], scale_table[:].indirect(offs_sb[:]))
        nc.vector.tensor_copy(x_scale_rows[:].bitcast(I32), picked_scales[:].bitcast(I32))
        for i in range(1, QUADRANT // BLOCK):
            nc.sync.dma_start(
                x_scale_rows[i:P:QUADRANT, :].bitcast(I32), picked_scales[BLOCK * i : P : QUADRANT, :].bitcast(I32)
            )
        mem_rows = mem.rearrange("(p t) u -> p t u", t=PACK)
        w2_rows = w2.rearrange("(p j) c -> p j c", j=PACK)
        nc.sync.dma_start(mem_sb[0][:], mem_rows[:, 0, :])
        nc.sync.dma_start(w2_first_raw[:], w2_rows[:, :, :P])
        nc.sync.dma_start(gn_sb[:], gn.rearrange("(p t) o -> p (t o)", t=PACK))

        w1_codes = placed("w1_codes", [P, H], U32, 7 * ROW)
        w1_scale_rows = tile("w1_scale_rows", [P, H], U8)
        nc.vector.tensor_copy(
            w1_grouped[:].rearrange("p (t m j) -> p m j t", t=PACK, j=PACK),
            w1_raw[:].rearrange("p j (m t) -> p m j t", t=PACK),
        )
        nc.sync.dma_start(mem_sb[1][:], mem_rows[:, 1, :])
        nc.sync.dma_start(mem_sb[2][:], mem_rows[:, 2, :])
        nc.vector.quantize_mx(w1_codes[:].bitcast(FP8X4), w1_scale_rows[:], w1_grouped[:])

        w2_first_grouped = placed("w2_first_grouped", [P, PACK * P], BF16, 4 * ROW)
        w2_grouped = placed("w2_grouped", [P, PACK * (N - P)], BF16, 9 * ROW - ROW // 8)
        w2_codes = tile("w2_codes", [P, N], U32)
        w2_scale_rows = placed("w2_scale_rows", [P, N], U8, 9 * ROW + 5 * ROW // 8)
        x_codes = tile("x_codes", [P, S], U32)
        y = {}
        y_gate = [tile("y_gate%d" % t, [P, S], F32) for t in range(PACK)]
        first_gate = placed("first_gate", [P, HALF], F32, 4 * ROW)
        gated1 = [tile("gated1_%d" % t, [P, S], F32) for t in range(2)]
        gated1.append(placed("gated1_2", [P, S], F32, 11 * ROW))
        gated1.append(placed("gated1_3", [P, S], F32, 9 * ROW + ROW // 2))
        h = {t: tile("h%d" % t, [P, S], F32) for t in (0, 1, 3)}
        h[2] = placed("h2", [P, S], F32, 12 * ROW)
        h_gate = [tile("h_gate%d" % t, [P, S], F32) for t in range(PACK)]
        early_slots = placed("early_slots", [P, 3 * S], F32, 7 * ROW)
        earliest_slots = tile("earliest_slots", [P, HALF], F32)
        late_slots = placed("late_slots", [P, S], F32, 10 * ROW - ROW // 8)
        gained_h = tile("gained_h", [P, PACK, S], F32)
        gated2 = [placed("gated2_%d" % g, [P, PACK * HALF], F32, (11 + g) * ROW) for g in range(2)]
        z_grouped, z_codes, z_scale_rows = {}, {}, {}

        def slots2(t, j0, n):
            if t == 0 and j0 < HALF:
                return earliest_slots[:, j0 : j0 + n]
            if t < 2:
                return early_slots[:, t * S + j0 : t * S + j0 + n]
            if j0 < HALF:
                return early_slots[:, 2 * S + (t - 2) * HALF + j0 : 2 * S + (t - 2) * HALF + j0 + n]
            return late_slots[:, (t - 3) * HALF + j0 : (t - 3) * HALF + j0 + n]

        def y_gate_cols(t, j0, n):
            return (first_gate if t == 0 and j0 < HALF else y_gate[t])[:, j0 : j0 + n]

        def woven(grouped):
            return grouped.rearrange("p (c i t) -> p c t i", i=2, t=PACK)

        def by_pairs(quarters):
            return quarters.rearrange("p t (c i) -> p c t i", i=2)

        def project(t, j0, n, bank, pieces=1):
            y[t, j0] = psum.tile([P, n], F32, name="y%d_%d" % (t, j0), tag="bank%d" % bank)
            nc.tensor.matmul_mx(
                y[t, j0][:],
                lhsT=w1_codes[:, t * P : (t + 1) * P].bitcast(FP8X4),
                lhsT_scale=w1_scale_rows[:, t * P : (t + 1) * P],
                rhs=x_codes[:, j0 : j0 + n].bitcast(FP8X4),
                rhs_scale=x_scale_rows[:, j0 : j0 + n],
                start=True,
                stop=True,
            )
            width = n // pieces
            for c0 in range(0, n, width):
                nc.scalar.activation(y_gate_cols(t, j0 + c0, width), y[t, j0][:, c0 : c0 + width], SIGMOID)

        def gate_first_slots(t, j0, n, slots=None):
            if slots is None:
                slots = mem_sb[t][:].indirect(entries(a1_sb, j0, n))
            nc.vector.tensor_tensor(gated1[t][:, j0 : j0 + n], slots, y_gate_cols(t, j0, n), MULT)

        def add_first_slots(t, j0, n, p0=None):
            p0 = j0 if p0 is None else p0
            nc.vector.tensor_tensor(
                h[t][:, j0 : j0 + n], y[t, p0][:, j0 - p0 : j0 - p0 + n], gated1[t][:, j0 : j0 + n], ADD
            )

        def gate(t, j0, n):
            nc.scalar.activation(h_gate[t][:, j0 : j0 + n], h[t][:, j0 : j0 + n], SIGMOID)

        def fetch_second_slots(t, j0, n):
            nc.scalar.activation(slots2(t, j0, n), mem_sb[t][:].indirect(entries(a2_sb, j0, n)), COPY)

        def gain_h(t, j0, n):
            cols = slice(j0, j0 + n)
            nc.scalar.activation(gained_h[:, t, cols], h[t][:, cols], COPY, scale=gn_sb[:, t : t + 1])

        def gain_h_aside(t):
            nc.gpsimd.tensor_scalar(gained_h[:, t, :], h[t][:], gn_sb[:, t : t + 1], 0.0, MULT, ADD)

        def chunk_of_gated2(j0, n):
            c0 = j0 % HALF
            return gated2[j0 // HALF][:, PACK * c0 : PACK * (c0 + n)].rearrange("p (t c) -> p t c", t=PACK)

        def gate_second_slots(t, j0, n):
            slots, gates = slots2(t, j0, n), h_gate[t][:, j0 : j0 + n]
            if j0 == HALF and n == HALF:
                both = gated2[1][:].rearrange("p (g t c) -> p t g c", g=2, t=PACK)
                gated = both[:, t, :, :]
                slots, gates = (x.rearrange("p (g c) -> p g c", g=2) for x in (slots, gates))
            else:
                gated = chunk_of_gated2(j0, n)[:, t, :]
            nc.vector.scalar_tensor_tensor(gated, slots, gn_sb[:, t : t + 1], gates, MULT, MULT)

        def close_second_hop(j0, n):
            z_grouped[j0] = placed("z_grouped%d" % j0, [P, PACK * n], BF16, 6 * ROW + 2 * PACK * j0)
            nc.vector.tensor_tensor(
                woven(z_grouped[j0][:]),
                by_pairs(gained_h[:, :, j0 : j0 + n]),
                by_pairs(chunk_of_gated2(j0, n)),
                ADD,
            )

        def group_w2(b, blocks, copy):
            c0, n = (b - 1) * P, blocks * P
            copy(woven(w2_grouped[:, c0 * PACK : (c0 + n) * PACK]), by_pairs(w2_raw[:, :, c0 : c0 + n]))

        def group_first_w2():
            nc.gpsimd.tensor_scalar(
                woven(w2_first_grouped[:]),
                by_pairs(w2_first_raw[:]),
                1.0,
                0.0,
                MULT,
                ADD,
            )

        def quantise_w2(b, blocks):
            cols = slice(b * P, (b + blocks) * P)
            grouped = w2_grouped[:, (b - 1) * P * PACK : (b - 1 + blocks) * P * PACK] if b else w2_first_grouped[:]
            nc.vector.quantize_mx(w2_codes[:, cols].bitcast(FP8X4), w2_scale_rows[:, cols], grouped)

        def quantise(j0, n):
            z_codes[j0] = tile("z_codes%d" % j0, [P, n], U32)
            z_scale_rows[j0] = tile("z_scale_rows%d" % j0, [P, n], U8)
            nc.vector.quantize_mx(z_codes[j0][:].bitcast(FP8X4), z_scale_rows[j0][:], z_grouped[j0][:])

        def multiply(j0, n, blocks, bank):
            acc = psum.tile([P, len(blocks), n], F32, name="acc%d_%d" % (j0, blocks[0]), tag="bank%d" % bank)
            for i, b in enumerate(blocks):
                nc.tensor.matmul_mx(
                    acc[:, i, :],
                    lhsT=w2_codes[:, b * P : (b + 1) * P].bitcast(FP8X4),
                    lhsT_scale=w2_scale_rows[:, b * P : (b + 1) * P],
                    rhs=z_codes[j0][:].bitcast(FP8X4),
                    rhs_scale=z_scale_rows[j0][:],
                    start=True,
                    stop=True,
                )
            return acc

        def store(j0, n, pair, rows):
            nc.sync.dma_start(
                out[2 * pair * P : 2 * (pair + 1) * P, j0 : j0 + n].rearrange("(b p) j -> p b j", p=P), rows[:]
            )

        def result(name, n):
            return tile(name, [P, 2, n], F32)

        for j0 in (0, HALF):
            nc.vector.tensor_copy(
                x_codes[:, j0 : j0 + HALF], word_table[:].bitcast(U32).indirect(entries(offs_sb, j0, HALF))
            )
        nc.sync.dma_start(mem_sb[3][:], mem_rows[:, 3, :])
        nc.sync.dma_start(w2_raw[:], w2_rows[:, :, P:])
        for piece, bank in enumerate((0, 5, 4, 6)):
            project(0, piece * P, P, bank)
        fetch_second_slots(0, 0, HALF)
        project(1, 0, S, 1, 2)
        for t in (2, 3):
            project(t, 0, S, t)

        first_slots = tile("first_slots", [P, HALF], F32)
        nc.vector.tensor_copy(first_slots[:], mem_sb[0][:].indirect(entries(a1_sb, HALF, HALF)))
        gate_first_slots(0, 0, P)
        gate_first_slots(0, P, P)
        gate_first_slots(0, HALF, P, first_slots[:, :P])
        gate_first_slots(0, HALF + P, P, first_slots[:, P:])
        for j0 in range(0, S, P):
            add_first_slots(0, j0, P)
        for t in range(1, PACK):
            for j0 in (0, HALF):
                gate_first_slots(t, j0, HALF)
            for j0 in (0, HALF):
                add_first_slots(t, j0, HALF, 0)
        group_first_w2()
        for t in range(PACK - 1):
            gain_h_aside(t)

        on_scalar, on_vector = nc.scalar.copy, nc.vector.tensor_copy
        fetch_second_slots(0, HALF, HALF)
        gate(0, 0, S)
        fetch_second_slots(1, 0, S)
        fetch_second_slots(2, 0, HALF)
        fetch_second_slots(3, 0, HALF)
        gate(1, 0, S)
        gate(2, 0, S)
        gate(3, 0, HALF)
        gain_h(3, 0, HALF)
        fetch_second_slots(3, HALF, HALF)
        gate(3, HALF, HALF)
        group_w2(2, 2, on_scalar)
        fetch_second_slots(2, HALF, HALF)
        gain_h(3, HALF, HALF)

        middle, last = HALF, HALF + P
        for t in range(PACK):
            gate_second_slots(t, 0, HALF)
        group_w2(1, 1, on_vector)
        close_second_hop(0, HALF)
        quantise_w2(0, 1)
        quantise_w2(1, 1)
        quantise(0, HALF)
        for t in (0, 1, 3):
            gate_second_slots(t, middle, P)
        quantise_w2(2, 2)
        gate_second_slots(2, middle, P)
        gate_second_slots(0, last, P)
        gate_second_slots(1, last, P)
        close_second_hop(middle, P)
        gate_second_slots(2, last, P)
        gate_second_slots(3, last, P)
        quantise(middle, P)
        close_second_hop(last, P)
        quantise(last, P)
        for pair, bank in enumerate((5, 6)):
            rows = result("a%d" % pair, HALF)
            on_scalar(rows[:], multiply(0, HALF, (2 * pair, 2 * pair + 1), bank)[:])
            store(0, HALF, pair, rows)
        for pair, bank in enumerate((7, 1)):
            rows = result("b%d" % pair, P)
            on_scalar(rows[:], multiply(HALF, P, (2 * pair, 2 * pair + 1), bank)[:])
            store(HALF, P, pair, rows)
        for pair, banks in enumerate(((0, 4), (2, 3))):
            rows = result("c%d" % pair, P)
            for i, copy in enumerate((on_scalar, on_vector)):
                copy(rows[:, i : i + 1, :], multiply(HALF + P, P, (2 * pair + i,), banks[i])[:])
            store(HALF + P, P, pair, rows)
